import numpy as np
import ml_dtypes


def mxq(x, axis, fmt="e4m3"):
    dtype, down = {"e4m3": (ml_dtypes.float8_e4m3fn, 7), "e5m2": (ml_dtypes.float8_e5m2, 14)}[fmt]
    v = np.moveaxis(np.asarray(x, np.float32).astype(ml_dtypes.bfloat16).astype(np.float64), axis, -1)
    blocks = v.reshape(v.shape[:-1] + (-1, 32))
    amax = np.abs(blocks).max(-1, keepdims=True)
    byte = np.maximum(np.where(amax > 0, np.frexp(amax)[1] - 1 + 127, 0) - down, 1)
    scale = np.exp2(byte - 127.0)
    codes = (blocks / scale).astype(np.float32).astype(dtype).astype(np.float64)
    return np.moveaxis((codes * scale).reshape(v.shape), -1, axis)


WIDE = False


def mx_kscale(k):
    if not WIDE:
        return np.ones(k)
    levels = np.array([10, -10, 5, -5, 0])
    if k % 512:
        return np.exp2(np.random.permutation(np.resize(levels, k // 32))).repeat(32)
    a = np.empty((k // 512, 16))
    for p in range(k // 512):
        a[p, :8] = np.random.permutation(np.resize(levels, 8))
        for g in range(8):
            far = levels[np.abs(levels - a[p, g]) >= 10]
            a[p, g + 8] = far[np.random.randint(len(far))]
    return np.exp2(a.ravel()).repeat(32)


def f64(x):
    return np.asarray(x).astype(np.float64)


def striped(idx):
    return np.tile(idx.reshape(-1, 16).T, (8, 1)).astype(np.uint16)


def unstriped(offs):
    return offs[:16].T.reshape(-1).astype(np.int64)


E2M1 = np.array([0.0, 0.5, 1.0, 1.5, 2.0, 3.0, 4.0, 6.0, -0.0, -0.5, -1.0, -1.5, -2.0, -3.0, -4.0, -6.0])


def pack_weight(w, fmt):
    k, n = w.shape
    w = f64(np.asarray(w, np.float32).astype(ml_dtypes.bfloat16)).reshape(k // 32, 32, n)
    amax = np.abs(w).max(1)
    if fmt == "e4m3":
        byte = np.frexp(amax)[1] - 1 + 127 - 7
    else:
        mant, ex = np.frexp(amax / 6.0)
        byte = np.where(mant > 0.5, ex, ex - 1) + 127
    byte = np.clip(np.where(amax > 0, byte, 1), 1, 254)
    scaled = (w * np.exp2(127.0 - byte)[:, None, :]).reshape(k, n).astype(np.float32)
    by_word = np.ascontiguousarray(scaled.reshape(k // 512, 128, 4, n).transpose(0, 1, 3, 2))
    if fmt == "e4m3":
        words = by_word.astype(ml_dtypes.float8_e4m3fn).view(np.uint8)
    else:
        c = by_word.astype(ml_dtypes.float4_e2m1fn).view(np.uint8) & 0xF
        words = (c[..., 0::2] | (c[..., 1::2] << 4)).reshape(k // 512, 128, 2 * n)
    return np.ascontiguousarray(words), np.ascontiguousarray(byte.astype(np.uint8).reshape(k // 512, 16, n))


def unpack_weight(words, scales, fmt):
    g, _, n = scales.shape
    words = np.ascontiguousarray(words).reshape(g, 128, n, -1)
    if fmt == "e4m3":
        vals = words.view(ml_dtypes.float8_e4m3fn).astype(np.float64)
    else:
        nib = np.empty((g, 128, n, 4), np.uint8)
        nib[..., 0::2] = words & 0xF
        nib[..., 1::2] = words >> 4
        vals = E2M1[nib]
    vals = vals * np.repeat(np.exp2(scales.astype(np.float64) - 127.0), 8, axis=1)[..., None]
    return vals.transpose(0, 1, 3, 2).reshape(g * 512, n)


def planes(y):
    n, m = y.shape
    v = y.astype(np.float32).astype(ml_dtypes.bfloat16).astype(np.float64).reshape(n // 32, 32, m)
    top = np.abs(v).max(1)
    byte = np.clip(np.where(top > 0, np.frexp(top)[1] - 1 + 127 - 7, 1), 1, 254)
    codes = (v * np.exp2(127.0 - byte)[:, None, :]).reshape(n, m).astype(np.float32).astype(ml_dtypes.float8_e4m3fn).view(np.uint8)
    words = codes.reshape(n // 512, 128, 4, m).transpose(0, 1, 3, 2)
    return np.ascontiguousarray(words), np.ascontiguousarray(byte.astype(np.uint8).reshape(n // 512, 16, m))


K, T, E, B, H, N = 512, 768, 8, 6, 512, 512


def setup_inputs():
    n = np.random.standard_normal
    s = mx_kscale(K)
    u = mx_kscale(H)
    slot_token = np.random.permutation(T)[:128 * B]
    block = np.sort(np.random.randint(E, size=B))
    x = pack_weight(n((K, T)) * s[:, None], "e4m3")
    wa = pack_weight(n((K, E * H)) / np.sqrt(K) / s[:, None] * np.tile(u, E), "e4m3")
    wb = pack_weight(n((H, E * N)) / np.sqrt(H) / u[:, None], "e4m3")
    return {
        "x_words": x[0],
        "x_scales": x[1],
        "w": (n((K, N)) / np.sqrt(K) / s[:, None]).astype(np.float32),
        "wa_words": wa[0],
        "wa_scales": wa[1],
        "wb_words": wb[0],
        "wb_scales": wb[1],
        "gate": (np.tile(np.random.uniform(0.2, 1.0, 128 * B), (128, 1))).astype(np.float32),
        "offs": striped(slot_token),
        "offs2": striped((block[:, None] * H + np.arange(H)).reshape(-1)),
        "offs3": striped((block[:, None] * N + np.arange(N)).reshape(-1)),
    }


def reference(x_words, x_scales, w, wa_words, wa_scales, wb_words, wb_scales, gate, offs, offs2, offs3):
    wq = mxq(f64(w), 0, "e4m3")
    idx, idx2, idx3 = unstriped(offs), unstriped(offs2), unstriped(offs3)
    x = unpack_weight(x_words, x_scales, "e4m3")
    out = wq.T @ x
    wa = unpack_weight(wa_words, wa_scales, "e4m3")[:, idx2]
    wb = unpack_weight(wb_words, wb_scales, "e4m3")[:, idx3]
    xq = x[:, idx]
    h = np.concatenate([wa[:, m * H:(m + 1) * H].T @ xq[:, 128 * m:128 * m + 128] for m in range(B)], axis=1)
    hq = mxq(h, 0, "e4m3")
    y = np.concatenate([wb[:, m * N:(m + 1) * N].T @ hq[:, 128 * m:128 * m + 128] for m in range(B)], axis=1)
    out[:, idx] += f64(gate[:1]) * y
    out_0 = out
    return (out_0,) + planes(out_0)

@@ -1,0 +1,207 @@
+from contextlib import ExitStack
+
+import concourse.mybir as mybir
+from concourse.masks import make_identity
+
+K, T, E, B, H, N = 512, 768, 8, 6, 512, 512
+FLOPS = 2 * K * N * T + 2 * K * H * T + 2 * H * N * T
+
+F32 = mybir.dt.float32
+BF16 = mybir.dt.bfloat16
+I32 = mybir.dt.int32
+U32 = mybir.dt.uint32
+U16 = mybir.dt.uint16
+U8 = mybir.dt.uint8
+FP8X4 = mybir.dt.float8_e4m3fn_x4
+COPY = mybir.ActivationFunctionType.Copy
+ADD = mybir.AluOpType.add
+
+P = 128
+PACK = 4
+SLOTS = 128
+HALF = T // 2
+PER_COL = 16
+
+
+def load_words(queue, tile, words):
+    queue.dma_start(out=tile[:], in_=words[0].rearrange("p c d -> p (c d)").bitcast(I32))
+
+
+def load_scale_rows(queue, plane, scales):
+    rows = scales[0].bitcast(I32)
+    view = plane[:].bitcast(I32)
+    for r in range(4):
+        queue.dma_start(out=view[r:P:32, :], in_=rows[r:16:4, :])
+
+
+def gather(nc, out, window, offsets, first, count):
+    cols = slice(first // PER_COL, (first + count) // PER_COL)
+    nc.vector.tensor_copy(out, window.indirect(offsets[:, cols]))
+
+
+def tile_moe_dyl_none_kernel(
+    tc, x_words, x_scales, w, wa_words, wa_scales, wb_words, wb_scales, gate, offs, offs2, offs3,
+    out_0, out_1, out_2,
+):
+    nc = tc.nc
+    with ExitStack() as ctx:
+        keep = ctx.enter_context(tc.tile_pool(name="keep", bufs=1))
+        ring = ctx.enter_context(tc.tile_pool(name="ring", bufs=2))
+        psum = ctx.enter_context(tc.psum_pool(name="psum", bufs=2))
+
+        tok_list = keep.tile([P, T // PER_COL], U16)
+        a_list = keep.tile([P, B * H // PER_COL], U16)
+        b_list = keep.tile([P, B * N // PER_COL], U16)
+        x_win = keep.tile([P, T], I32, align_bytes=64)
+        xs_win = keep.tile([P, T], U8, align_bytes=64)
+        a_win = keep.tile([P, E * H], I32, align_bytes=64)
+        as_win = keep.tile([P, E * H], U8, align_bytes=64)
+        b_win = keep.tile([P, E * N], I32, align_bytes=64)
+        bs_win = keep.tile([P, E * N], U8, align_bytes=64)
+        w_raw = keep.tile([P, PACK, N], F32, align_bytes=64)
+        gate_col = keep.tile([P, B], F32)
+        ident = keep.tile([P, P], F32, align_bytes=64)
+
+        nc.vector.memset(as_win[:].bitcast(I32), 0)
+        nc.gpsimd.memset(xs_win[:].bitcast(I32), 0)
+        nc.vector.memset(bs_win[:].bitcast(I32), 0)
+        make_identity(nc, ident[:])
+
+        nc.sync.dma_start(tok_list[:], offs)
+        load_words(nc.sync, x_win, x_words)
+        nc.sync.dma_start(a_list[:], offs2)
+        load_scale_rows(nc.sync, as_win, wa_scales)
+        load_scale_rows(nc.sync, xs_win, x_scales)
+        load_words(nc.sync, a_win, wa_words)
+        nc.sync.dma_start(out=w_raw[:], in_=w.rearrange("(p j) n -> p j n", j=PACK))
+        nc.sync.dma_start(b_list[:], offs3)
+        load_scale_rows(nc.sync, bs_win, wb_scales)
+        load_words(nc.sync, b_win, wb_words)
+        with nc.allow_non_contiguous_dma(reason="one gate value for each slot's partition"):
+            nc.sync.dma_start(out=gate_col[:], in_=gate[0:1, :].rearrange("o (m u) -> u (o m)", u=SLOTS))
+
+        xg = keep.tile([P, T], I32, align_bytes=64)
+        xsg = keep.tile([P, T], U8, align_bytes=64)
+        asg = [keep.tile([P, 3 * H], U8, align_bytes=64, name="asg%d" % h) for h in range(2)]
+        bsg = [keep.tile([P, 3 * N], U8, align_bytes=64, name="bsg%d" % h) for h in range(2)]
+        ag = [keep.tile([P, 2 * H], I32, align_bytes=64, name="ag%d" % q) for q in range(3)]
+        bg = [keep.tile([P, 2 * N], I32, align_bytes=64, name="bg%d" % q) for q in range(3)]
+
+        for h in range(2):
+            gather(nc, xg[:, h * HALF:(h + 1) * HALF].bitcast(U32), x_win[:].bitcast(U32), tok_list, h * HALF, HALF)
+        for h in range(2):
+            gather(nc, asg[h][:], as_win[:], a_list, h * 3 * H, 3 * H)
+        for h in range(2):
+            gather(nc, xsg[:, h * HALF:(h + 1) * HALF], xs_win[:], tok_list, h * HALF, HALF)
+
+        w_bf = keep.tile([P, N * PACK], BF16, align_bytes=64)
+        nc.scalar.copy(
+            out=w_bf[:].rearrange("p (t m j) -> p m t j", t=PACK, j=PACK),
+            in_=w_raw[:].rearrange("p j (m t) -> p m t j", t=PACK),
+        )
+        wq = keep.tile([P, N], I32, align_bytes=64)
+        wqs = keep.tile([P, N], U8, align_bytes=64)
+        nc.vector.quantize_mx(out=wq[:].bitcast(FP8X4), scales=wqs[:], in_=w_bf[:])
+        base = [keep.tile([P, PACK, HALF], F32, align_bytes=64, name="base%d" % h) for h in range(2)]
+        for t in range(PACK):
+            cols = slice(t * P, (t + 1) * P)
+            for h in range(2):
+                acc = psum.tile([P, HALF], F32, tag="mm", name="base_acc")
+                for s0, s1 in ((0, 256), (256, HALF)):
+                    sl = slice(h * HALF + s0, h * HALF + s1)
+                    nc.tensor.matmul_mx(
+                        out=acc[:, s0:s1], lhsT=wq[:, cols].bitcast(FP8X4), lhsT_scale=wqs[:, cols],
+                        rhs=xg[:, sl].bitcast(FP8X4), rhs_scale=xsg[:, sl], start=True, stop=True,
+                    )
+                nc.scalar.copy(out=base[h][:, t, :], in_=acc[:])
+
+        hq = [keep.tile([P, SLOTS], I32, align_bytes=64, name="hq%d" % m) for m in range(B)]
+        hqs = [keep.tile([P, SLOTS], U8, align_bytes=64, name="hqs%d" % m) for m in range(B)]
+        gated = [keep.tile([P, PACK, HALF], F32, align_bytes=64, name="gated%d" % h) for h in range(2)]
+
+        def first_layer(m):
+            slots = slice(m * SLOTS, (m + 1) * SLOTS)
+            wc = slice((m % 2) * H, (m % 2 + 1) * H)
+            sc = slice((m % 3) * H, (m % 3 + 1) * H)
+            h_acc = psum.tile([P, H], F32, tag="mm", name="h_acc")
+            nc.tensor.matmul_mx(
+                out=h_acc[:], lhsT=xg[:, slots].bitcast(FP8X4), lhsT_scale=xsg[:, slots],
+                rhs=ag[m // 2][:, wc].bitcast(FP8X4), rhs_scale=asg[m // 3][:, sc], start=True, stop=True,
+            )
+            h_bf = ring.tile([P, H], BF16, align_bytes=64)
+            nc.scalar.copy(
+                out=h_bf[:].rearrange("s (u p e) -> s u p e", u=2, e=2),
+                in_=h_acc[:].rearrange("s (p u e) -> s u p e", u=2, e=2),
+            )
+            h_turn = psum.tile([P, 2, SLOTS], F32, tag="h_turn")
+            pairs = h_bf[:].bitcast(F32)
+            for u in range(2):
+                nc.tensor.transpose(h_turn[:, u, :], pairs[:, u * P:(u + 1) * P], ident[:])
+            h_grp = ring.tile([P, SLOTS * PACK], BF16, align_bytes=64)
+            nc.scalar.copy(
+                out=h_grp[:].bitcast(F32).rearrange("p (s u) -> p s u", u=2),
+                in_=h_turn[:].rearrange("p u s -> p s u"),
+            )
+            nc.vector.quantize_mx(out=hq[m][:].bitcast(FP8X4), scales=hqs[m][:], in_=h_grp[:])
+
+        def second_layer(m):
+            wc = slice((m % 2) * N, (m % 2 + 1) * N)
+            sc = slice((m % 3) * N, (m % 3 + 1) * N)
+            y_acc = psum.tile([P, N], F32, tag="y_acc")
+            nc.tensor.matmul_mx(
+                out=y_acc[:], lhsT=hq[m][:].bitcast(FP8X4), lhsT_scale=hqs[m][:],
+                rhs=bg[m // 2][:, wc].bitcast(FP8X4), rhs_scale=bsg[m // 3][:, sc], start=True, stop=True,
+            )
+            y_sb = ring.tile([P, PACK, P], F32, align_bytes=64)
+            nc.scalar.activation(
+                out=y_sb[:], in_=y_acc[:].rearrange("s (p t) -> s t p", t=PACK), func=COPY,
+                scale=gate_col[:, m:m + 1],
+            )
+            y_turn = psum.tile([P, PACK, SLOTS], F32, tag="y_turn")
+            for t in range(PACK):
+                nc.tensor.transpose(y_turn[:, t, :], y_sb[:, t, :], ident[:])
+            s0 = (m % 3) * SLOTS
+            nc.scalar.copy(out=gated[m // 3][:, :, s0:s0 + SLOTS], in_=y_turn[:])
+
+        for q in range(3):
+            gather(nc, ag[q][:].bitcast(U32), a_win[:].bitcast(U32), a_list, q * 2 * H, 2 * H)
+            first_layer(2 * q)
+            first_layer(2 * q + 1)
+        for h in range(2):
+            gather(nc, bsg[h][:], bs_win[:], b_list, h * 3 * N, 3 * N)
+        for q in range(3):
+            gather(nc, bg[q][:].bitcast(U32), b_win[:].bitcast(U32), b_list, q * 2 * N, 2 * N)
+            second_layer(2 * q)
+            second_layer(2 * q + 1)
+
+        result = [keep.tile([P, T], F32, align_bytes=64, name="result%d" % t) for t in range(PACK)]
+        chunks = ((0, 512), (512, T))
+        rounded = [keep.tile([P, c1 - c0, PACK], BF16, align_bytes=64, name="rounded%d" % c0) for c0, c1 in chunks]
+        out_rows = out_0.rearrange("(p t) c -> p t c", t=PACK)
+        for h in range(2):
+            cols = slice(h * HALF // PER_COL, (h + 1) * HALF // PER_COL)
+            for t in range(PACK):
+                nc.vector.tensor_tensor(
+                    result[t][:].indirect(tok_list[:, cols]), gated[h][:, t, :], base[h][:, t, :], ADD,
+                )
+        for t in range(PACK):
+            nc.sync.dma_start(out=out_rows[:, t, :], in_=result[t][:])
+            for i, (c0, c1) in enumerate(chunks):
+                nc.scalar.copy(out=rounded[i][:, :, t], in_=result[t][:, c0:c1])
+
+        out_scales = keep.tile([P, T], U8, align_bytes=64)
+        out_words = out_1[0].rearrange("p c d -> p (c d)").bitcast(I32)
+        for i, (c0, c1) in enumerate(chunks):
+            codes = keep.tile([P, c1 - c0], I32, align_bytes=64, name="codes%d" % c0)
+            nc.vector.quantize_mx(
+                out=codes[:].bitcast(FP8X4), scales=out_scales[:, c0:c1],
+                in_=rounded[i][:].rearrange("p c t -> p (c t)"),
+            )
+            nc.sync.dma_start(out=out_words[:, c0:c1], in_=codes[:])
+        scale_rows = out_2[0].bitcast(I32)
+        for quad in range(4):
+            queue = nc.sync if quad % 2 == 0 else nc.scalar
+            queue.dma_start(
+                out=scale_rows[4 * quad:4 * quad + 4, :],
+                in_=out_scales[:].bitcast(I32)[32 * quad:32 * quad + 4, :],
+            )

@@ -21,15 +21,16 @@ PACK = 4
 SLOTS = 128
 HALF = T // 2
 PER_COL = 16
+X_WINDOW = 1024
 
 
 def load_words(queue, tile, words):
-    queue.dma_start(out=tile[:], in_=words[0].rearrange("p c d -> p (c d)").bitcast(I32))
+    queue.dma_start(out=tile, in_=words[0].rearrange("p c d -> p (c d)").bitcast(I32))
 
 
 def load_scale_rows(queue, plane, scales):
     rows = scales[0].bitcast(I32)
-    view = plane[:].bitcast(I32)
+    view = plane.bitcast(I32)
     for r in range(4):
         queue.dma_start(out=view[r:P:32, :], in_=rows[r:16:4, :])
 
@@ -52,81 +53,86 @@ def tile_moe_dyl_none_kernel(
         tok_list = keep.tile([P, T // PER_COL], U16)
         a_list = keep.tile([P, B * H // PER_COL], U16)
         b_list = keep.tile([P, B * N // PER_COL], U16)
-        x_win = keep.tile([P, T], I32, align_bytes=64)
-        xs_win = keep.tile([P, T], U8, align_bytes=64)
-        a_win = keep.tile([P, E * H], I32, align_bytes=64)
-        as_win = keep.tile([P, E * H], U8, align_bytes=64)
-        b_win = keep.tile([P, E * N], I32, align_bytes=64)
+        x_win = keep.tile([P, X_WINDOW], I32, align_bytes=64, tag="x_then_a")
+        xs_win = keep.tile([P, X_WINDOW], U8, align_bytes=64, tag="xs_then_gate")
+        as_win = keep.tile([P, E * H], U8, align_bytes=64, tag="as_then_ag")
         bs_win = keep.tile([P, E * N], U8, align_bytes=64)
-        w_raw = keep.tile([P, PACK, N], F32, align_bytes=64)
-        gate_col = keep.tile([P, B], F32)
+        w_raw = keep.tile([P, PACK, N], F32, align_bytes=64, tag="w_then_b")
         ident = keep.tile([P, P], F32, align_bytes=64)
 
-        nc.vector.memset(as_win[:].bitcast(I32), 0)
         nc.gpsimd.memset(xs_win[:].bitcast(I32), 0)
+        nc.vector.memset(as_win[:].bitcast(I32), 0)
+        nc.gpsimd.memset(x_win[:, T:], 0)
         nc.vector.memset(bs_win[:].bitcast(I32), 0)
         make_identity(nc, ident[:])
 
         nc.sync.dma_start(tok_list[:], offs)
-        load_words(nc.sync, x_win, x_words)
+        load_words(nc.sync, x_win[:, :T], x_words)
         nc.sync.dma_start(a_list[:], offs2)
-        load_scale_rows(nc.sync, as_win, wa_scales)
-        load_scale_rows(nc.sync, xs_win, x_scales)
-        load_words(nc.sync, a_win, wa_words)
-        nc.sync.dma_start(out=w_raw[:], in_=w.rearrange("(p j) n -> p j n", j=PACK))
         nc.sync.dma_start(b_list[:], offs3)
-        load_scale_rows(nc.sync, bs_win, wb_scales)
-        load_words(nc.sync, b_win, wb_words)
-        with nc.allow_non_contiguous_dma(reason="one gate value for each slot's partition"):
-            nc.sync.dma_start(out=gate_col[:], in_=gate[0:1, :].rearrange("o (m u) -> u (o m)", u=SLOTS))
+        load_scale_rows(nc.scalar, xs_win[:, :T], x_scales)
+        load_scale_rows(nc.scalar, as_win[:], wa_scales)
+        nc.sync.dma_start(out=w_raw[:], in_=w.rearrange("(p j) n -> p j n", j=PACK))
+        load_scale_rows(nc.sync, bs_win[:], wb_scales)
 
         xg = keep.tile([P, T], I32, align_bytes=64)
         xsg = keep.tile([P, T], U8, align_bytes=64)
-        asg = [keep.tile([P, 3 * H], U8, align_bytes=64, name="asg%d" % h) for h in range(2)]
-        bsg = [keep.tile([P, 3 * N], U8, align_bytes=64, name="bsg%d" % h) for h in range(2)]
-        ag = [keep.tile([P, 2 * H], I32, align_bytes=64, name="ag%d" % q) for q in range(3)]
-        bg = [keep.tile([P, 2 * N], I32, align_bytes=64, name="bg%d" % q) for q in range(3)]
+        gather(nc, xg[:].bitcast(U32), x_win[:].bitcast(U32), tok_list, 0, T)
+        gather(nc, xsg[:], xs_win[:], tok_list, 0, T)
+        a_win = keep.tile([P, E * H], I32, align_bytes=64, tag="x_then_a")
+        load_words(nc.sync, a_win[:], wa_words)
 
-        for h in range(2):
-            gather(nc, xg[:, h * HALF:(h + 1) * HALF].bitcast(U32), x_win[:].bitcast(U32), tok_list, h * HALF, HALF)
-        for h in range(2):
-            gather(nc, asg[h][:], as_win[:], a_list, h * 3 * H, 3 * H)
-        for h in range(2):
-            gather(nc, xsg[:, h * HALF:(h + 1) * HALF], xs_win[:], tok_list, h * HALF, HALF)
+        asg = [keep.tile([P, 3 * H], U8, align_bytes=64, name="asg0")]
+        gather(nc, asg[0][:], as_win[:], a_list, 0, 3 * H)
 
-        w_bf = keep.tile([P, N * PACK], BF16, align_bytes=64)
+        w_bf = keep.tile([P, N * PACK], BF16, align_bytes=64, tag="wbf_then_as")
         nc.scalar.copy(
             out=w_bf[:].rearrange("p (t m j) -> p m t j", t=PACK, j=PACK),
             in_=w_raw[:].rearrange("p j (m t) -> p m t j", t=PACK),
         )
+        b_win = keep.tile([P, E * N], I32, align_bytes=64, tag="w_then_b")
+        load_words(nc.sync, b_win[:], wb_words)
         wq = keep.tile([P, N], I32, align_bytes=64)
         wqs = keep.tile([P, N], U8, align_bytes=64)
         nc.vector.quantize_mx(out=wq[:].bitcast(FP8X4), scales=wqs[:], in_=w_bf[:])
-        base = [keep.tile([P, PACK, HALF], F32, align_bytes=64, name="base%d" % h) for h in range(2)]
-        for t in range(PACK):
-            cols = slice(t * P, (t + 1) * P)
-            for h in range(2):
-                acc = psum.tile([P, HALF], F32, tag="mm", name="base_acc")
-                for s0, s1 in ((0, 256), (256, HALF)):
-                    sl = slice(h * HALF + s0, h * HALF + s1)
-                    nc.tensor.matmul_mx(
-                        out=acc[:, s0:s1], lhsT=wq[:, cols].bitcast(FP8X4), lhsT_scale=wqs[:, cols],
-                        rhs=xg[:, sl].bitcast(FP8X4), rhs_scale=xsg[:, sl], start=True, stop=True,
-                    )
-                nc.scalar.copy(out=base[h][:, t, :], in_=acc[:])
+        asg.append(keep.tile([P, 3 * H], U8, align_bytes=64, name="asg1", tag="wbf_then_as"))
+        gather(nc, asg[1][:], as_win[:], a_list, 3 * H, 3 * H)
+        gate_col = keep.tile([P, B], F32, align_bytes=64, tag="xs_then_gate")
+        with nc.allow_non_contiguous_dma(reason="one gate value for each slot's partition"):
+            nc.sync.dma_start(out=gate_col[:], in_=gate[0:1, :].rearrange("o (m u) -> u (o m)", u=SLOTS))
 
+        base = keep.tile([P, PACK, T], F32, align_bytes=64)
+
+        def frozen(acc, t, s0, s1):
+            cols = slice(t * P, (t + 1) * P)
+            nc.tensor.matmul_mx(
+                out=acc, lhsT=wq[:, cols].bitcast(FP8X4), lhsT_scale=wqs[:, cols],
+                rhs=xg[:, s0:s1].bitcast(FP8X4), rhs_scale=xsg[:, s0:s1], start=True, stop=True,
+            )
+
+        for t in range(PACK):
+            acc = psum.tile([P, 512], F32, tag="mm", name="base_acc")
+            frozen(acc[:], t, 0, 512)
+            nc.scalar.copy(out=base[:, t, 0:512], in_=acc[:])
+        for t in range(0, PACK, 2):
+            acc = psum.tile([P, 2, T - 512], F32, tag="mm", name="base_acc")
+            for u in range(2):
+                frozen(acc[:, u, :], t + u, 512, T)
+            nc.scalar.copy(out=base[:, t:t + 2, 512:T], in_=acc[:])
+
+        ag = keep.tile([P, B * H], I32, align_bytes=64, tag="as_then_ag")
         hq = [keep.tile([P, SLOTS], I32, align_bytes=64, name="hq%d" % m) for m in range(B)]
         hqs = [keep.tile([P, SLOTS], U8, align_bytes=64, name="hqs%d" % m) for m in range(B)]
-        gated = [keep.tile([P, PACK, HALF], F32, align_bytes=64, name="gated%d" % h) for h in range(2)]
+        gated = keep.tile([P, PACK, T], F32, align_bytes=64)
+        bg, bsg = [], []
 
         def first_layer(m):
             slots = slice(m * SLOTS, (m + 1) * SLOTS)
-            wc = slice((m % 2) * H, (m % 2 + 1) * H)
             sc = slice((m % 3) * H, (m % 3 + 1) * H)
             h_acc = psum.tile([P, H], F32, tag="mm", name="h_acc")
             nc.tensor.matmul_mx(
                 out=h_acc[:], lhsT=xg[:, slots].bitcast(FP8X4), lhsT_scale=xsg[:, slots],
-                rhs=ag[m // 2][:, wc].bitcast(FP8X4), rhs_scale=asg[m // 3][:, sc], start=True, stop=True,
+                rhs=ag[:, m * H:(m + 1) * H].bitcast(FP8X4), rhs_scale=asg[m // 3][:, sc], start=True, stop=True,
             )
             h_bf = ring.tile([P, H], BF16, align_bytes=64)
             nc.scalar.copy(
@@ -137,7 +143,7 @@ def tile_moe_dyl_none_kernel(
             pairs = h_bf[:].bitcast(F32)
             for u in range(2):
                 nc.tensor.transpose(h_turn[:, u, :], pairs[:, u * P:(u + 1) * P], ident[:])
-            h_grp = ring.tile([P, SLOTS * PACK], BF16, align_bytes=64)
+            h_grp = keep.tile([P, SLOTS * PACK], BF16, align_bytes=64, tag="h_grp%d" % m)
             nc.scalar.copy(
                 out=h_grp[:].bitcast(F32).rearrange("p (s u) -> p s u", u=2),
                 in_=h_turn[:].rearrange("p u s -> p s u"),
@@ -145,12 +151,11 @@ def tile_moe_dyl_none_kernel(
             nc.vector.quantize_mx(out=hq[m][:].bitcast(FP8X4), scales=hqs[m][:], in_=h_grp[:])
 
         def second_layer(m):
-            wc = slice((m % 2) * N, (m % 2 + 1) * N)
             sc = slice((m % 3) * N, (m % 3 + 1) * N)
             y_acc = psum.tile([P, N], F32, tag="y_acc")
             nc.tensor.matmul_mx(
                 out=y_acc[:], lhsT=hq[m][:].bitcast(FP8X4), lhsT_scale=hqs[m][:],
-                rhs=bg[m // 2][:, wc].bitcast(FP8X4), rhs_scale=bsg[m // 3][:, sc], start=True, stop=True,
+                rhs=bg[m // 3][:, sc].bitcast(FP8X4), rhs_scale=bsg[m // 3][:, sc], start=True, stop=True,
             )
             y_sb = ring.tile([P, PACK, P], F32, align_bytes=64)
             nc.scalar.activation(
@@ -160,42 +165,63 @@ def tile_moe_dyl_none_kernel(
             y_turn = psum.tile([P, PACK, SLOTS], F32, tag="y_turn")
             for t in range(PACK):
                 nc.tensor.transpose(y_turn[:, t, :], y_sb[:, t, :], ident[:])
-            s0 = (m % 3) * SLOTS
-            nc.scalar.copy(out=gated[m // 3][:, :, s0:s0 + SLOTS], in_=y_turn[:])
+            nc.scalar.copy(out=gated[:, :, m * SLOTS:(m + 1) * SLOTS], in_=y_turn[:])
 
-        for q in range(3):
-            gather(nc, ag[q][:].bitcast(U32), a_win[:].bitcast(U32), a_list, q * 2 * H, 2 * H)
-            first_layer(2 * q)
-            first_layer(2 * q + 1)
         for h in range(2):
-            gather(nc, bsg[h][:], bs_win[:], b_list, h * 3 * N, 3 * N)
-        for q in range(3):
-            gather(nc, bg[q][:].bitcast(U32), b_win[:].bitcast(U32), b_list, q * 2 * N, 2 * N)
-            second_layer(2 * q)
-            second_layer(2 * q + 1)
+            gather(nc, ag[:, h * 3 * H:(h + 1) * 3 * H].bitcast(U32), a_win[:].bitcast(U32), a_list, h * 3 * H, 3 * H)
+        bsg.append(keep.tile([P, 3 * N], U8, align_bytes=64, name="bsg0", tag="x_then_a"))
+        gather(nc, bsg[0][:], bs_win[:], b_list, 0, 3 * N)
+        for m in range(3):
+            first_layer(m)
+        bg.append(keep.tile([P, 3 * N], I32, align_bytes=64, name="bg0", tag="h_grp2"))
+        gather(nc, bg[0][:].bitcast(U32), b_win[:].bitcast(U32), b_list, 0, 3 * N)
+        first_layer(3)
+        bsg.append(keep.tile([P, 3 * N], U8, align_bytes=64, name="bsg1", tag="h_grp3"))
+        gather(nc, bsg[1][:], bs_win[:], b_list, 3 * N, 3 * N)
+        first_layer(4)
+        first_layer(5)
+        bg.append(keep.tile([P, 3 * N], I32, align_bytes=64, name="bg1", tag="h_grp5"))
+        gather(nc, bg[1][:].bitcast(U32), b_win[:].bitcast(U32), b_list, 3 * N, 3 * N)
+        for m in range(B):
+            second_layer(m)
 
-        result = [keep.tile([P, T], F32, align_bytes=64, name="result%d" % t) for t in range(PACK)]
-        chunks = ((0, 512), (512, T))
-        rounded = [keep.tile([P, c1 - c0, PACK], BF16, align_bytes=64, name="rounded%d" % c0) for c0, c1 in chunks]
-        out_rows = out_0.rearrange("(p t) c -> p t c", t=PACK)
+        last = PACK - 1
+        result = [
+            keep.tile([P, 2 * T if t == last else T], F32, align_bytes=64, name="result%d" % t) for t in range(PACK)
+        ]
         for h in range(2):
             cols = slice(h * HALF // PER_COL, (h + 1) * HALF // PER_COL)
-            for t in range(PACK):
+            slots = slice(h * HALF, (h + 1) * HALF)
+            for t in range(last):
                 nc.vector.tensor_tensor(
-                    result[t][:].indirect(tok_list[:, cols]), gated[h][:, t, :], base[h][:, t, :], ADD,
+                    result[t][:].indirect(tok_list[:, cols]), gated[:, t, slots], base[:, t, slots], ADD,
                 )
+        nc.vector.tensor_tensor(result[last][:].indirect(tok_list[:]), gated[:, last, :], base[:, last, :], ADD)
+
+        CUT = 512
+        woven = keep.tile([P, CUT, PACK], BF16, align_bytes=64)
+        planes = keep.tile([P, PACK, T - CUT], BF16, align_bytes=64)
+        woven_rest = keep.tile([P, T - CUT, PACK], BF16, align_bytes=64)
+        out_rows = out_0.rearrange("(p t) c -> p t c", t=PACK)
         for t in range(PACK):
-            nc.sync.dma_start(out=out_rows[:, t, :], in_=result[t][:])
-            for i, (c0, c1) in enumerate(chunks):
-                nc.scalar.copy(out=rounded[i][:, :, t], in_=result[t][:, c0:c1])
+            nc.sync.dma_start(out=out_rows[:, t, :], in_=result[t][:, :T])
+            nc.scalar.copy(out=woven[:, :, t], in_=result[t][:, :CUT])
+            if t == last:
+                nc.vector.tensor_copy(out=planes[:, t, :], in_=result[t][:, CUT:T])
+            else:
+                nc.scalar.copy(out=planes[:, t, :], in_=result[t][:, CUT:T])
+        nc.vector.tensor_copy(
+            out=woven_rest[:].rearrange("p (c i) t -> p c t i", i=4),
+            in_=planes[:].rearrange("p t (c i) -> p c t i", i=4),
+        )
 
         out_scales = keep.tile([P, T], U8, align_bytes=64)
         out_words = out_1[0].rearrange("p c d -> p (c d)").bitcast(I32)
-        for i, (c0, c1) in enumerate(chunks):
+        for src, c0, c1 in ((woven_rest, CUT, T), (woven, 0, CUT)):
             codes = keep.tile([P, c1 - c0], I32, align_bytes=64, name="codes%d" % c0)
             nc.vector.quantize_mx(
                 out=codes[:].bitcast(FP8X4), scales=out_scales[:, c0:c1],
-                in_=rounded[i][:].rearrange("p c t -> p (c t)"),
+                in_=src[:].rearrange("p c t -> p (c t)"),
             )
             nc.sync.dma_start(out=out_words[:, c0:c1], in_=codes[:])
         scale_rows = out_2[0].bitcast(I32)

@@ -49,6 +49,7 @@ def tile_moe_dyl_none_kernel(
         keep = ctx.enter_context(tc.tile_pool(name="keep", bufs=1))
         ring = ctx.enter_context(tc.tile_pool(name="ring", bufs=2))
         psum = ctx.enter_context(tc.psum_pool(name="psum", bufs=2))
+        banks = ctx.enter_context(tc.psum_pool(name="banks", bufs=1))
 
         tok_list = keep.tile([P, T // PER_COL], U16)
         a_list = keep.tile([P, B * H // PER_COL], U16)
@@ -60,9 +61,9 @@ def tile_moe_dyl_none_kernel(
         w_raw = keep.tile([P, PACK, N], F32, align_bytes=64, tag="w_then_b")
         ident = keep.tile([P, P], F32, align_bytes=64)
 
-        nc.gpsimd.memset(xs_win[:].bitcast(I32), 0)
         nc.vector.memset(as_win[:].bitcast(I32), 0)
         nc.gpsimd.memset(x_win[:, T:], 0)
+        nc.vector.memset(xs_win[:].bitcast(I32), 0)
         nc.vector.memset(bs_win[:].bitcast(I32), 0)
         make_identity(nc, ident[:])
 
@@ -70,20 +71,20 @@ def tile_moe_dyl_none_kernel(
         load_words(nc.sync, x_win[:, :T], x_words)
         nc.sync.dma_start(a_list[:], offs2)
         nc.sync.dma_start(b_list[:], offs3)
-        load_scale_rows(nc.scalar, xs_win[:, :T], x_scales)
-        load_scale_rows(nc.scalar, as_win[:], wa_scales)
         nc.sync.dma_start(out=w_raw[:], in_=w.rearrange("(p j) n -> p j n", j=PACK))
+        load_scale_rows(nc.scalar, as_win[:], wa_scales)
+        load_scale_rows(nc.sync, xs_win[:, :T], x_scales)
         load_scale_rows(nc.sync, bs_win[:], wb_scales)
 
         xg = keep.tile([P, T], I32, align_bytes=64)
         xsg = keep.tile([P, T], U8, align_bytes=64)
         gather(nc, xg[:].bitcast(U32), x_win[:].bitcast(U32), tok_list, 0, T)
-        gather(nc, xsg[:], xs_win[:], tok_list, 0, T)
         a_win = keep.tile([P, E * H], I32, align_bytes=64, tag="x_then_a")
         load_words(nc.sync, a_win[:], wa_words)
 
         asg = [keep.tile([P, 3 * H], U8, align_bytes=64, name="asg0")]
         gather(nc, asg[0][:], as_win[:], a_list, 0, 3 * H)
+        gather(nc, xsg[:], xs_win[:], tok_list, 0, T)
 
         w_bf = keep.tile([P, N * PACK], BF16, align_bytes=64, tag="wbf_then_as")
         nc.scalar.copy(
@@ -121,12 +122,12 @@ def tile_moe_dyl_none_kernel(
             nc.scalar.copy(out=base[:, t:t + 2, 512:T], in_=acc[:])
 
         ag = keep.tile([P, B * H], I32, align_bytes=64, tag="as_then_ag")
-        hq = [keep.tile([P, SLOTS], I32, align_bytes=64, name="hq%d" % m) for m in range(B)]
-        hqs = [keep.tile([P, SLOTS], U8, align_bytes=64, name="hqs%d" % m) for m in range(B)]
+        hq = [keep.tile([P, 2 * SLOTS], I32, align_bytes=64, name="hq%d" % q) for q in range(3)]
+        hqs = [keep.tile([P, 2 * SLOTS], U8, align_bytes=64, name="hqs%d" % q) for q in range(3)]
         gated = keep.tile([P, PACK, T], F32, align_bytes=64)
         bg, bsg = [], []
 
-        def first_layer(m):
+        def first_layer(m, h_grp):
             slots = slice(m * SLOTS, (m + 1) * SLOTS)
             sc = slice((m % 3) * H, (m % 3 + 1) * H)
             h_acc = psum.tile([P, H], F32, tag="mm", name="h_acc")
@@ -143,87 +144,100 @@ def tile_moe_dyl_none_kernel(
             pairs = h_bf[:].bitcast(F32)
             for u in range(2):
                 nc.tensor.transpose(h_turn[:, u, :], pairs[:, u * P:(u + 1) * P], ident[:])
-            h_grp = keep.tile([P, SLOTS * PACK], BF16, align_bytes=64, tag="h_grp%d" % m)
             nc.scalar.copy(
-                out=h_grp[:].bitcast(F32).rearrange("p (s u) -> p s u", u=2),
+                out=h_grp.bitcast(F32).rearrange("p (s u) -> p s u", u=2),
                 in_=h_turn[:].rearrange("p u s -> p s u"),
             )
-            nc.vector.quantize_mx(out=hq[m][:].bitcast(FP8X4), scales=hqs[m][:], in_=h_grp[:])
+
+        def first_pair(q):
+            width = SLOTS * PACK
+            h_grp = keep.tile([P, 2 * width], BF16, align_bytes=64, tag="h_grp%d" % q)
+            for i in range(2):
+                first_layer(2 * q + i, h_grp[:, i * width:(i + 1) * width])
+            nc.vector.quantize_mx(out=hq[q][:].bitcast(FP8X4), scales=hqs[q][:], in_=h_grp[:])
 
         def second_layer(m):
-            sc = slice((m % 3) * N, (m % 3 + 1) * N)
-            y_acc = psum.tile([P, N], F32, tag="y_acc")
+            part, i = (0, m) if m < 2 else (1, m - 2)
+            sc = slice(i * N, (i + 1) * N)
+            hc = slice((m % 2) * SLOTS, (m % 2 + 1) * SLOTS)
+            y_acc = banks.tile([P, N], F32, tag="ACCDCD"[m])
             nc.tensor.matmul_mx(
-                out=y_acc[:], lhsT=hq[m][:].bitcast(FP8X4), lhsT_scale=hqs[m][:],
-                rhs=bg[m // 3][:, sc].bitcast(FP8X4), rhs_scale=bsg[m // 3][:, sc], start=True, stop=True,
+                out=y_acc[:], lhsT=hq[m // 2][:, hc].bitcast(FP8X4), lhsT_scale=hqs[m // 2][:, hc],
+                rhs=bg[part][:, sc].bitcast(FP8X4), rhs_scale=bsg[part][:, sc], start=True, stop=True,
             )
             y_sb = ring.tile([P, PACK, P], F32, align_bytes=64)
             nc.scalar.activation(
                 out=y_sb[:], in_=y_acc[:].rearrange("s (p t) -> s t p", t=PACK), func=COPY,
                 scale=gate_col[:, m:m + 1],
             )
-            y_turn = psum.tile([P, PACK, SLOTS], F32, tag="y_turn")
+            y_turn = banks.tile([P, PACK, SLOTS], F32, tag="BDABAB"[m])
             for t in range(PACK):
                 nc.tensor.transpose(y_turn[:, t, :], y_sb[:, t, :], ident[:])
             nc.scalar.copy(out=gated[:, :, m * SLOTS:(m + 1) * SLOTS], in_=y_turn[:])
 
-        for h in range(2):
-            gather(nc, ag[:, h * 3 * H:(h + 1) * 3 * H].bitcast(U32), a_win[:].bitcast(U32), a_list, h * 3 * H, 3 * H)
-        bsg.append(keep.tile([P, 3 * N], U8, align_bytes=64, name="bsg0", tag="x_then_a"))
-        gather(nc, bsg[0][:], bs_win[:], b_list, 0, 3 * N)
-        for m in range(3):
-            first_layer(m)
-        bg.append(keep.tile([P, 3 * N], I32, align_bytes=64, name="bg0", tag="h_grp2"))
-        gather(nc, bg[0][:].bitcast(U32), b_win[:].bitcast(U32), b_list, 0, 3 * N)
-        first_layer(3)
-        bsg.append(keep.tile([P, 3 * N], U8, align_bytes=64, name="bsg1", tag="h_grp3"))
-        gather(nc, bsg[1][:], bs_win[:], b_list, 3 * N, 3 * N)
-        first_layer(4)
-        first_layer(5)
-        bg.append(keep.tile([P, 3 * N], I32, align_bytes=64, name="bg1", tag="h_grp5"))
-        gather(nc, bg[1][:].bitcast(U32), b_win[:].bitcast(U32), b_list, 3 * N, 3 * N)
+        gather(nc, ag[:, :2 * H].bitcast(U32), a_win[:].bitcast(U32), a_list, 0, 2 * H)
+        gather(nc, ag[:, 2 * H:].bitcast(U32), a_win[:].bitcast(U32), a_list, 2 * H, 4 * H)
+        bsg.append(keep.tile([P, 2 * N], U8, align_bytes=64, name="bsg0", tag="x_then_a"))
+        gather(nc, bsg[0][:], bs_win[:], b_list, 0, 2 * N)
+        first_pair(0)
+        bg.append(keep.tile([P, 2 * N], I32, align_bytes=64, name="bg0", tag="h_grp0"))
+        gather(nc, bg[0][:].bitcast(U32), b_win[:].bitcast(U32), b_list, 0, 2 * N)
+        first_pair(1)
+        bsg.append(keep.tile([P, 4 * N], U8, align_bytes=64, name="bsg1", tag="h_grp1"))
+        gather(nc, bsg[1][:], bs_win[:], b_list, 2 * N, 4 * N)
+        first_pair(2)
+        bg.append(keep.tile([P, 4 * N], I32, align_bytes=64, name="bg1", tag="h_grp2"))
+        for i in range(2):
+            gather(nc, bg[1][:, i * 2 * N:(i + 1) * 2 * N].bitcast(U32), b_win[:].bitcast(U32), b_list, (i + 1) * 2 * N, 2 * N)
         for m in range(B):
             second_layer(m)
 
         last = PACK - 1
         result = [
-            keep.tile([P, 2 * T if t == last else T], F32, align_bytes=64, name="result%d" % t) for t in range(PACK)
+            keep.tile([P, T if t < 2 else X_WINDOW], F32, align_bytes=64, name="result%d" % t) for t in range(PACK)
         ]
-        for h in range(2):
-            cols = slice(h * HALF // PER_COL, (h + 1) * HALF // PER_COL)
-            slots = slice(h * HALF, (h + 1) * HALF)
-            for t in range(last):
-                nc.vector.tensor_tensor(
-                    result[t][:].indirect(tok_list[:, cols]), gated[:, t, slots], base[:, t, slots], ADD,
-                )
-        nc.vector.tensor_tensor(result[last][:].indirect(tok_list[:]), gated[:, last, :], base[:, last, :], ADD)
 
-        CUT = 512
-        woven = keep.tile([P, CUT, PACK], BF16, align_bytes=64)
-        planes = keep.tile([P, PACK, T - CUT], BF16, align_bytes=64)
-        woven_rest = keep.tile([P, T - CUT, PACK], BF16, align_bytes=64)
+        def scatter(t, s0, s1):
+            nc.vector.tensor_tensor(
+                result[t][:].indirect(tok_list[:, s0 // PER_COL:s1 // PER_COL]),
+                gated[:, t, s0:s1], base[:, t, s0:s1], ADD,
+            )
+
+        for t in range(PACK):
+            scatter(t, 0, 256)
+        for t in range(2):
+            scatter(t, 256, 512)
+        for t in range(2):
+            scatter(t, 512, T)
+        for t in range(2, PACK):
+            scatter(t, 256, T)
+
+        C = T // 3
+        woven = [keep.tile([P, C, PACK], BF16, align_bytes=64, name="woven%d" % c) for c in range(3)]
+        planes = keep.tile([P, PACK, C], BF16, align_bytes=64)
         out_rows = out_0.rearrange("(p t) c -> p t c", t=PACK)
         for t in range(PACK):
             nc.sync.dma_start(out=out_rows[:, t, :], in_=result[t][:, :T])
-            nc.scalar.copy(out=woven[:, :, t], in_=result[t][:, :CUT])
+            for c in range(2):
+                nc.scalar.copy(out=woven[c][:, :, t], in_=result[t][:, c * C:(c + 1) * C])
             if t == last:
-                nc.vector.tensor_copy(out=planes[:, t, :], in_=result[t][:, CUT:T])
+                nc.vector.tensor_copy(out=planes[:, t, :], in_=result[t][:, 2 * C:T])
             else:
-                nc.scalar.copy(out=planes[:, t, :], in_=result[t][:, CUT:T])
+                nc.scalar.copy(out=planes[:, t, :], in_=result[t][:, 2 * C:T])
         nc.vector.tensor_copy(
-            out=woven_rest[:].rearrange("p (c i) t -> p c t i", i=4),
+            out=woven[2][:].rearrange("p (c i) t -> p c t i", i=4),
             in_=planes[:].rearrange("p t (c i) -> p c t i", i=4),
         )
 
         out_scales = keep.tile([P, T], U8, align_bytes=64)
         out_words = out_1[0].rearrange("p c d -> p (c d)").bitcast(I32)
-        for src, c0, c1 in ((woven_rest, CUT, T), (woven, 0, CUT)):
-            codes = keep.tile([P, c1 - c0], I32, align_bytes=64, name="codes%d" % c0)
+        for c in (0, 2, 1):
+            codes = keep.tile([P, C], I32, align_bytes=64, name="codes%d" % c)
             nc.vector.quantize_mx(
-                out=codes[:].bitcast(FP8X4), scales=out_scales[:, c0:c1],
-                in_=src[:].rearrange("p c t -> p (c t)"),
+                out=codes[:].bitcast(FP8X4), scales=out_scales[:, c * C:(c + 1) * C],
+                in_=woven[c][:].rearrange("p c t -> p (c t)"),
             )
-            nc.sync.dma_start(out=out_words[:, c0:c1], in_=codes[:])
+            nc.sync.dma_start(out=out_words[:, c * C:(c + 1) * C], in_=codes[:])
         scale_rows = out_2[0].bitcast(I32)
         for quad in range(4):
             queue = nc.sync if quad % 2 == 0 else nc.scalar

@@ -1,7 +1,6 @@
 from contextlib import ExitStack
 
 import concourse.mybir as mybir
-from concourse.masks import make_identity
 
 K, T, E, B, H, N = 512, 768, 8, 6, 512, 512
 FLOPS = 2 * K * N * T + 2 * K * H * T + 2 * H * N * T
@@ -19,20 +18,21 @@ ADD = mybir.AluOpType.add
 P = 128
 PACK = 4
 SLOTS = 128
-HALF = T // 2
+PAIRS = B // 2
 PER_COL = 16
-X_WINDOW = 1024
+WINDOW = 1024
+A_ROW, B_ROW = 4, 8
 
 
 def load_words(queue, tile, words):
     queue.dma_start(out=tile, in_=words[0].rearrange("p c d -> p (c d)").bitcast(I32))
 
 
-def load_scale_rows(queue, plane, scales):
+def load_scale_rows(queue, plane, scales, first_row):
     rows = scales[0].bitcast(I32)
     view = plane.bitcast(I32)
     for r in range(4):
-        queue.dma_start(out=view[r:P:32, :], in_=rows[r:16:4, :])
+        queue.dma_start(out=view[first_row + r:P:32, :], in_=rows[r:16:4, :])
 
 
 def gather(nc, out, window, offsets, first, count):
@@ -48,59 +48,69 @@ def tile_moe_dyl_none_kernel(
     with ExitStack() as ctx:
         keep = ctx.enter_context(tc.tile_pool(name="keep", bufs=1))
         ring = ctx.enter_context(tc.tile_pool(name="ring", bufs=2))
+        shared = ctx.enter_context(tc.tile_pool(name="shared", bufs=1))
         psum = ctx.enter_context(tc.psum_pool(name="psum", bufs=2))
-        banks = ctx.enter_context(tc.psum_pool(name="banks", bufs=1))
 
         tok_list = keep.tile([P, T // PER_COL], U16)
         a_list = keep.tile([P, B * H // PER_COL], U16)
         b_list = keep.tile([P, B * N // PER_COL], U16)
-        x_win = keep.tile([P, X_WINDOW], I32, align_bytes=64, tag="x_then_a")
-        xs_win = keep.tile([P, X_WINDOW], U8, align_bytes=64, tag="xs_then_gate")
-        as_win = keep.tile([P, E * H], U8, align_bytes=64, tag="as_then_ag")
+        x_win = keep.tile([P, WINDOW], I32, align_bytes=64, tag="x_then_gate")
+        xs_win = keep.tile([P, WINDOW], U8, align_bytes=64)
+        as_win = keep.tile([P, E * H], U8, align_bytes=64)
         bs_win = keep.tile([P, E * N], U8, align_bytes=64)
-        w_raw = keep.tile([P, PACK, N], F32, align_bytes=64, tag="w_then_b")
+        w_raw = shared.tile([P, PACK, N], F32, align_bytes=64, offset=0)
+        zeros = keep.tile([P, P], F32, align_bytes=64, tag="zeros_then_a")
         ident = keep.tile([P, P], F32, align_bytes=64)
 
+        nc.gpsimd.memset(xs_win[:].bitcast(I32), 0)
         nc.vector.memset(as_win[:].bitcast(I32), 0)
         nc.gpsimd.memset(x_win[:, T:], 0)
-        nc.vector.memset(xs_win[:].bitcast(I32), 0)
-        nc.vector.memset(bs_win[:].bitcast(I32), 0)
-        make_identity(nc, ident[:])
+        nc.gpsimd.memset(zeros[:], 0.0)
+        nc.gpsimd.affine_select(
+            out=ident[:], in_=zeros[:], compare_op=mybir.AluOpType.not_equal, fill=1.0, base=0,
+            pattern=[[-1, P]], channel_multiplier=1,
+        )
+        nc.gpsimd.memset(bs_win[:].bitcast(I32), 0)
 
         nc.sync.dma_start(tok_list[:], offs)
         load_words(nc.sync, x_win[:, :T], x_words)
+        load_scale_rows(nc.sync, xs_win[:, :T], x_scales, 0)
         nc.sync.dma_start(a_list[:], offs2)
-        nc.sync.dma_start(b_list[:], offs3)
         nc.sync.dma_start(out=w_raw[:], in_=w.rearrange("(p j) n -> p j n", j=PACK))
-        load_scale_rows(nc.scalar, as_win[:], wa_scales)
-        load_scale_rows(nc.sync, xs_win[:, :T], x_scales)
-        load_scale_rows(nc.sync, bs_win[:], wb_scales)
+        nc.sync.dma_start(b_list[:], offs3)
+        load_scale_rows(nc.scalar, as_win[:], wa_scales, A_ROW)
+        a_win = keep.tile([P, E * H], I32, align_bytes=64, tag="zeros_then_a")
+        load_words(nc.sync, a_win[:], wa_words)
+        load_scale_rows(nc.sync, bs_win[:], wb_scales, B_ROW)
 
         xg = keep.tile([P, T], I32, align_bytes=64)
         xsg = keep.tile([P, T], U8, align_bytes=64)
-        gather(nc, xg[:].bitcast(U32), x_win[:].bitcast(U32), tok_list, 0, T)
-        a_win = keep.tile([P, E * H], I32, align_bytes=64, tag="x_then_a")
-        load_words(nc.sync, a_win[:], wa_words)
-
-        asg = [keep.tile([P, 3 * H], U8, align_bytes=64, name="asg0")]
-        gather(nc, asg[0][:], as_win[:], a_list, 0, 3 * H)
         gather(nc, xsg[:], xs_win[:], tok_list, 0, T)
+        gather(nc, xg[:].bitcast(U32), x_win[:].bitcast(U32), tok_list, 0, T)
+        gate_col = keep.tile([P, B], F32, align_bytes=64, tag="x_then_gate")
+        with nc.allow_non_contiguous_dma(reason="one gate value for each slot's partition"):
+            nc.sync.dma_start(out=gate_col[:], in_=gate[0:1, :].rearrange("o (m u) -> u (o m)", u=SLOTS))
 
-        w_bf = keep.tile([P, N * PACK], BF16, align_bytes=64, tag="wbf_then_as")
+        asg = []
+
+        def gather_a_scales(q, tile):
+            asg.append(tile)
+            gather(nc, asg[q][:], as_win[:], a_list, q * 2 * H, 2 * H)
+
+        for q in range(2):
+            gather_a_scales(q, keep.tile([P, 2 * H], U8, align_bytes=64, name="asg%d" % q, tag="scales%d" % q))
+
+        w_bf = keep.tile([P, N * PACK], BF16, align_bytes=64, tag="wbf_then_b")
         nc.scalar.copy(
             out=w_bf[:].rearrange("p (t m j) -> p m t j", t=PACK, j=PACK),
             in_=w_raw[:].rearrange("p j (m t) -> p m t j", t=PACK),
         )
-        b_win = keep.tile([P, E * N], I32, align_bytes=64, tag="w_then_b")
-        load_words(nc.sync, b_win[:], wb_words)
         wq = keep.tile([P, N], I32, align_bytes=64)
         wqs = keep.tile([P, N], U8, align_bytes=64)
         nc.vector.quantize_mx(out=wq[:].bitcast(FP8X4), scales=wqs[:], in_=w_bf[:])
-        asg.append(keep.tile([P, 3 * H], U8, align_bytes=64, name="asg1", tag="wbf_then_as"))
-        gather(nc, asg[1][:], as_win[:], a_list, 3 * H, 3 * H)
-        gate_col = keep.tile([P, B], F32, align_bytes=64, tag="xs_then_gate")
-        with nc.allow_non_contiguous_dma(reason="one gate value for each slot's partition"):
-            nc.sync.dma_start(out=gate_col[:], in_=gate[0:1, :].rearrange("o (m u) -> u (o m)", u=SLOTS))
+        b_win = keep.tile([P, E * N], I32, align_bytes=64, tag="wbf_then_b")
+        load_words(nc.sync, b_win[:], wb_words)
+        gather_a_scales(2, shared.tile([P, 2 * H], U8, align_bytes=64, name="asg2", offset=0))
 
         base = keep.tile([P, PACK, T], F32, align_bytes=64)
 
@@ -121,19 +131,20 @@ def tile_moe_dyl_none_kernel(
                 frozen(acc[:, u, :], t + u, 512, T)
             nc.scalar.copy(out=base[:, t:t + 2, 512:T], in_=acc[:])
 
-        ag = keep.tile([P, B * H], I32, align_bytes=64, tag="as_then_ag")
-        hq = [keep.tile([P, 2 * SLOTS], I32, align_bytes=64, name="hq%d" % q) for q in range(3)]
-        hqs = [keep.tile([P, 2 * SLOTS], U8, align_bytes=64, name="hqs%d" % q) for q in range(3)]
+        ag = shared.tile([P, B * H], I32, align_bytes=64, offset=2 * H)
+        bg = keep.tile([P, B * N], I32, align_bytes=64)
+        hq = [keep.tile([P, 2 * SLOTS], I32, align_bytes=64, name="hq%d" % q) for q in range(PAIRS)]
+        hqs = [keep.tile([P, 2 * SLOTS], U8, align_bytes=64, name="hqs%d" % q) for q in range(PAIRS)]
         gated = keep.tile([P, PACK, T], F32, align_bytes=64)
-        bg, bsg = [], []
+        bsg = []
 
         def first_layer(m, h_grp):
             slots = slice(m * SLOTS, (m + 1) * SLOTS)
-            sc = slice((m % 3) * H, (m % 3 + 1) * H)
+            sc = slice((m % 2) * H, (m % 2 + 1) * H)
             h_acc = psum.tile([P, H], F32, tag="mm", name="h_acc")
             nc.tensor.matmul_mx(
                 out=h_acc[:], lhsT=xg[:, slots].bitcast(FP8X4), lhsT_scale=xsg[:, slots],
-                rhs=ag[:, m * H:(m + 1) * H].bitcast(FP8X4), rhs_scale=asg[m // 3][:, sc], start=True, stop=True,
+                rhs=ag[:, m * H:(m + 1) * H].bitcast(FP8X4), rhs_scale=asg[m // 2][A_ROW:, sc], start=True, stop=True,
             )
             h_bf = ring.tile([P, H], BF16, align_bytes=64)
             nc.scalar.copy(
@@ -151,51 +162,46 @@ def tile_moe_dyl_none_kernel(
 
         def first_pair(q):
             width = SLOTS * PACK
-            h_grp = keep.tile([P, 2 * width], BF16, align_bytes=64, tag="h_grp%d" % q)
+            h_grp = keep.tile([P, 2 * width], BF16, align_bytes=64, name="h_grp%d" % q)
             for i in range(2):
                 first_layer(2 * q + i, h_grp[:, i * width:(i + 1) * width])
             nc.vector.quantize_mx(out=hq[q][:].bitcast(FP8X4), scales=hqs[q][:], in_=h_grp[:])
 
+        def gather_b_scales(q):
+            bsg.append(keep.tile([P, 2 * N], U8, align_bytes=64, name="bsg%d" % q, tag="scales%d" % (q % 2)))
+            gather(nc, bsg[q][:], bs_win[:], b_list, q * 2 * N, 2 * N)
+
         def second_layer(m):
-            part, i = (0, m) if m < 2 else (1, m - 2)
-            sc = slice(i * N, (i + 1) * N)
+            sc = slice((m % 2) * N, (m % 2 + 1) * N)
             hc = slice((m % 2) * SLOTS, (m % 2 + 1) * SLOTS)
-            y_acc = banks.tile([P, N], F32, tag="ACCDCD"[m])
+            y_acc = psum.tile([P, N], F32, tag="y_acc")
             nc.tensor.matmul_mx(
                 out=y_acc[:], lhsT=hq[m // 2][:, hc].bitcast(FP8X4), lhsT_scale=hqs[m // 2][:, hc],
-                rhs=bg[part][:, sc].bitcast(FP8X4), rhs_scale=bsg[part][:, sc], start=True, stop=True,
+                rhs=bg[:, m * N:(m + 1) * N].bitcast(FP8X4), rhs_scale=bsg[m // 2][B_ROW:, sc], start=True, stop=True,
             )
             y_sb = ring.tile([P, PACK, P], F32, align_bytes=64)
             nc.scalar.activation(
                 out=y_sb[:], in_=y_acc[:].rearrange("s (p t) -> s t p", t=PACK), func=COPY,
                 scale=gate_col[:, m:m + 1],
             )
-            y_turn = banks.tile([P, PACK, SLOTS], F32, tag="BDABAB"[m])
+            y_turn = psum.tile([P, PACK, SLOTS], F32, tag="y_turn")
             for t in range(PACK):
                 nc.tensor.transpose(y_turn[:, t, :], y_sb[:, t, :], ident[:])
             nc.scalar.copy(out=gated[:, :, m * SLOTS:(m + 1) * SLOTS], in_=y_turn[:])
 
-        gather(nc, ag[:, :2 * H].bitcast(U32), a_win[:].bitcast(U32), a_list, 0, 2 * H)
-        gather(nc, ag[:, 2 * H:].bitcast(U32), a_win[:].bitcast(U32), a_list, 2 * H, 4 * H)
-        bsg.append(keep.tile([P, 2 * N], U8, align_bytes=64, name="bsg0", tag="x_then_a"))
-        gather(nc, bsg[0][:], bs_win[:], b_list, 0, 2 * N)
-        first_pair(0)
-        bg.append(keep.tile([P, 2 * N], I32, align_bytes=64, name="bg0", tag="h_grp0"))
-        gather(nc, bg[0][:].bitcast(U32), b_win[:].bitcast(U32), b_list, 0, 2 * N)
-        first_pair(1)
-        bsg.append(keep.tile([P, 4 * N], U8, align_bytes=64, name="bsg1", tag="h_grp1"))
-        gather(nc, bsg[1][:], bs_win[:], b_list, 2 * N, 4 * N)
-        first_pair(2)
-        bg.append(keep.tile([P, 4 * N], I32, align_bytes=64, name="bg1", tag="h_grp2"))
-        for i in range(2):
-            gather(nc, bg[1][:, i * 2 * N:(i + 1) * 2 * N].bitcast(U32), b_win[:].bitcast(U32), b_list, (i + 1) * 2 * N, 2 * N)
-        for m in range(B):
-            second_layer(m)
+        for q in range(PAIRS):
+            cols = slice(q * 2 * H, (q + 1) * 2 * H)
+            gather(nc, ag[:, cols].bitcast(U32), a_win[:].bitcast(U32), a_list, q * 2 * H, 2 * H)
+        for q in range(PAIRS):
+            first_pair(q)
+        for q in range(PAIRS):
+            cols = slice(q * 2 * N, (q + 1) * 2 * N)
+            gather_b_scales(q)
+            gather(nc, bg[:, cols].bitcast(U32), b_win[:].bitcast(U32), b_list, q * 2 * N, 2 * N)
+            second_layer(2 * q)
+            second_layer(2 * q + 1)
 
-        last = PACK - 1
-        result = [
-            keep.tile([P, T if t < 2 else X_WINDOW], F32, align_bytes=64, name="result%d" % t) for t in range(PACK)
-        ]
+        result = [keep.tile([P, WINDOW], F32, align_bytes=64, name="result%d" % t) for t in range(PACK)]
 
         def scatter(t, s0, s1):
             nc.vector.tensor_tensor(
@@ -205,33 +211,26 @@ def tile_moe_dyl_none_kernel(
 
         for t in range(PACK):
             scatter(t, 0, 256)
-        for t in range(2):
-            scatter(t, 256, 512)
-        for t in range(2):
-            scatter(t, 512, T)
-        for t in range(2, PACK):
+        for t in range(PACK):
             scatter(t, 256, T)
 
         C = T // 3
         woven = [keep.tile([P, C, PACK], BF16, align_bytes=64, name="woven%d" % c) for c in range(3)]
-        planes = keep.tile([P, PACK, C], BF16, align_bytes=64)
         out_rows = out_0.rearrange("(p t) c -> p t c", t=PACK)
         for t in range(PACK):
             nc.sync.dma_start(out=out_rows[:, t, :], in_=result[t][:, :T])
-            for c in range(2):
-                nc.scalar.copy(out=woven[c][:, :, t], in_=result[t][:, c * C:(c + 1) * C])
-            if t == last:
-                nc.vector.tensor_copy(out=planes[:, t, :], in_=result[t][:, 2 * C:T])
-            else:
-                nc.scalar.copy(out=planes[:, t, :], in_=result[t][:, 2 * C:T])
-        nc.vector.tensor_copy(
-            out=woven[2][:].rearrange("p (c i) t -> p c t i", i=4),
-            in_=planes[:].rearrange("p t (c i) -> p c t i", i=4),
-        )
+            for c in range(3):
+                values = result[t][:, c * C:(c + 1) * C]
+                if c > 0 and t == 2:
+                    nc.scalar.copy(out=woven[c][:, :, 2:4], in_=values.unsqueeze(2).to_broadcast([P, C, 2]))
+                elif c > 0 and t == 3:
+                    nc.vector.tensor_copy(out=woven[c][:, :, t], in_=values)
+                else:
+                    nc.scalar.copy(out=woven[c][:, :, t], in_=values)
 
         out_scales = keep.tile([P, T], U8, align_bytes=64)
         out_words = out_1[0].rearrange("p c d -> p (c d)").bitcast(I32)
-        for c in (0, 2, 1):
+        for c in (1, 0, 2):
             codes = keep.tile([P, C], I32, align_bytes=64, name="codes%d" % c)
             nc.vector.quantize_mx(
                 out=codes[:].bitcast(FP8X4), scales=out_scales[:, c * C:(c + 1) * C],

@@ -1,6 +1,7 @@
 from contextlib import ExitStack
 
 import concourse.mybir as mybir
+from concourse.masks import make_identity
 
 K, T, E, B, H, N = 512, 768, 8, 6, 512, 512
 FLOPS = 2 * K * N * T + 2 * K * H * T + 2 * H * N * T
@@ -49,47 +50,38 @@ def tile_moe_dyl_none_kernel(
         keep = ctx.enter_context(tc.tile_pool(name="keep", bufs=1))
         ring = ctx.enter_context(tc.tile_pool(name="ring", bufs=2))
         shared = ctx.enter_context(tc.tile_pool(name="shared", bufs=1))
-        psum = ctx.enter_context(tc.psum_pool(name="psum", bufs=2))
+        banks = ctx.enter_context(tc.psum_pool(name="banks", bufs=1))
 
         tok_list = keep.tile([P, T // PER_COL], U16)
         a_list = keep.tile([P, B * H // PER_COL], U16)
         b_list = keep.tile([P, B * N // PER_COL], U16)
-        x_win = keep.tile([P, WINDOW], I32, align_bytes=64, tag="x_then_gate")
+        x_win = keep.tile([P, WINDOW], I32, align_bytes=64, tag="x_then_a")
         xs_win = keep.tile([P, WINDOW], U8, align_bytes=64)
         as_win = keep.tile([P, E * H], U8, align_bytes=64)
         bs_win = keep.tile([P, E * N], U8, align_bytes=64)
-        w_raw = shared.tile([P, PACK, N], F32, align_bytes=64, offset=0)
-        zeros = keep.tile([P, P], F32, align_bytes=64, tag="zeros_then_a")
+        w_raw = shared.tile([P, PACK, N], F32, align_bytes=64, offset=11 * 1024)
         ident = keep.tile([P, P], F32, align_bytes=64)
 
-        nc.gpsimd.memset(xs_win[:].bitcast(I32), 0)
         nc.vector.memset(as_win[:].bitcast(I32), 0)
+        nc.vector.memset(xs_win[:].bitcast(I32), 0)
         nc.gpsimd.memset(x_win[:, T:], 0)
-        nc.gpsimd.memset(zeros[:], 0.0)
-        nc.gpsimd.affine_select(
-            out=ident[:], in_=zeros[:], compare_op=mybir.AluOpType.not_equal, fill=1.0, base=0,
-            pattern=[[-1, P]], channel_multiplier=1,
-        )
-        nc.gpsimd.memset(bs_win[:].bitcast(I32), 0)
+        nc.vector.memset(bs_win[:].bitcast(I32), 0)
+        make_identity(nc, ident[:])
 
         nc.sync.dma_start(tok_list[:], offs)
         load_words(nc.sync, x_win[:, :T], x_words)
-        load_scale_rows(nc.sync, xs_win[:, :T], x_scales, 0)
         nc.sync.dma_start(a_list[:], offs2)
-        nc.sync.dma_start(out=w_raw[:], in_=w.rearrange("(p j) n -> p j n", j=PACK))
         nc.sync.dma_start(b_list[:], offs3)
+        nc.sync.dma_start(out=w_raw[:], in_=w.rearrange("(p j) n -> p j n", j=PACK))
         load_scale_rows(nc.scalar, as_win[:], wa_scales, A_ROW)
-        a_win = keep.tile([P, E * H], I32, align_bytes=64, tag="zeros_then_a")
-        load_words(nc.sync, a_win[:], wa_words)
-        load_scale_rows(nc.sync, bs_win[:], wb_scales, B_ROW)
+        load_scale_rows(nc.sync, xs_win[:, :T], x_scales, 0)
+        load_scale_rows(nc.scalar, bs_win[:], wb_scales, B_ROW)
 
         xg = keep.tile([P, T], I32, align_bytes=64)
         xsg = keep.tile([P, T], U8, align_bytes=64)
-        gather(nc, xsg[:], xs_win[:], tok_list, 0, T)
         gather(nc, xg[:].bitcast(U32), x_win[:].bitcast(U32), tok_list, 0, T)
-        gate_col = keep.tile([P, B], F32, align_bytes=64, tag="x_then_gate")
-        with nc.allow_non_contiguous_dma(reason="one gate value for each slot's partition"):
-            nc.sync.dma_start(out=gate_col[:], in_=gate[0:1, :].rearrange("o (m u) -> u (o m)", u=SLOTS))
+        a_win = keep.tile([P, E * H], I32, align_bytes=64, tag="x_then_a")
+        load_words(nc.sync, a_win[:], wa_words)
 
         asg = []
 
@@ -99,8 +91,9 @@ def tile_moe_dyl_none_kernel(
 
         for q in range(2):
             gather_a_scales(q, keep.tile([P, 2 * H], U8, align_bytes=64, name="asg%d" % q, tag="scales%d" % q))
+        gather(nc, xsg[:], xs_win[:], tok_list, 0, T)
 
-        w_bf = keep.tile([P, N * PACK], BF16, align_bytes=64, tag="wbf_then_b")
+        w_bf = keep.tile([P, N * PACK], BF16, align_bytes=64, tag="wbf_then_gate")
         nc.scalar.copy(
             out=w_bf[:].rearrange("p (t m j) -> p m t j", t=PACK, j=PACK),
             in_=w_raw[:].rearrange("p j (m t) -> p m t j", t=PACK),
@@ -108,9 +101,12 @@ def tile_moe_dyl_none_kernel(
         wq = keep.tile([P, N], I32, align_bytes=64)
         wqs = keep.tile([P, N], U8, align_bytes=64)
         nc.vector.quantize_mx(out=wq[:].bitcast(FP8X4), scales=wqs[:], in_=w_bf[:])
-        b_win = keep.tile([P, E * N], I32, align_bytes=64, tag="wbf_then_b")
+        b_win = shared.tile([P, E * N], I32, align_bytes=64, offset=13 * 1024)
         load_words(nc.sync, b_win[:], wb_words)
-        gather_a_scales(2, shared.tile([P, 2 * H], U8, align_bytes=64, name="asg2", offset=0))
+        gate_col = keep.tile([P, B], F32, align_bytes=64, tag="wbf_then_gate")
+        with nc.allow_non_contiguous_dma(reason="one gate value for each slot's partition"):
+            nc.sync.dma_start(out=gate_col[:], in_=gate[0:1, :].rearrange("o (m u) -> u (o m)", u=SLOTS))
+        gather_a_scales(2, shared.tile([P, 2 * H], U8, align_bytes=64, name="asg2", offset=12 * 1024))
 
         base = keep.tile([P, PACK, T], F32, align_bytes=64)
 
@@ -122,16 +118,18 @@ def tile_moe_dyl_none_kernel(
             )
 
         for t in range(PACK):
-            acc = psum.tile([P, 512], F32, tag="mm", name="base_acc")
+            acc = banks.tile([P, 512], F32, tag="bank%d" % t, name="base_acc")
             frozen(acc[:], t, 0, 512)
             nc.scalar.copy(out=base[:, t, 0:512], in_=acc[:])
-        for t in range(0, PACK, 2):
-            acc = psum.tile([P, 2, T - 512], F32, tag="mm", name="base_acc")
-            for u in range(2):
-                frozen(acc[:, u, :], t + u, 512, T)
-            nc.scalar.copy(out=base[:, t:t + 2, 512:T], in_=acc[:])
 
-        ag = shared.tile([P, B * H], I32, align_bytes=64, offset=2 * H)
+        def frozen_rest():
+            for t in range(0, PACK, 2):
+                acc = banks.tile([P, 2, T - 512], F32, tag="bank%d" % (t // 2), name="rest_acc")
+                for u in range(2):
+                    frozen(acc[:, u, :], t + u, 512, T)
+                nc.scalar.copy(out=base[:, t:t + 2, 512:T], in_=acc[:])
+
+        ag = shared.tile([P, B * H], I32, align_bytes=64, offset=0)
         bg = keep.tile([P, B * N], I32, align_bytes=64)
         hq = [keep.tile([P, 2 * SLOTS], I32, align_bytes=64, name="hq%d" % q) for q in range(PAIRS)]
         hqs = [keep.tile([P, 2 * SLOTS], U8, align_bytes=64, name="hqs%d" % q) for q in range(PAIRS)]
@@ -141,7 +139,7 @@ def tile_moe_dyl_none_kernel(
         def first_layer(m, h_grp):
             slots = slice(m * SLOTS, (m + 1) * SLOTS)
             sc = slice((m % 2) * H, (m % 2 + 1) * H)
-            h_acc = psum.tile([P, H], F32, tag="mm", name="h_acc")
+            h_acc = banks.tile([P, H], F32, tag="bank%d" % (4 + m % 2), name="h_acc")
             nc.tensor.matmul_mx(
                 out=h_acc[:], lhsT=xg[:, slots].bitcast(FP8X4), lhsT_scale=xsg[:, slots],
                 rhs=ag[:, m * H:(m + 1) * H].bitcast(FP8X4), rhs_scale=asg[m // 2][A_ROW:, sc], start=True, stop=True,
@@ -151,7 +149,7 @@ def tile_moe_dyl_none_kernel(
                 out=h_bf[:].rearrange("s (u p e) -> s u p e", u=2, e=2),
                 in_=h_acc[:].rearrange("s (p u e) -> s u p e", u=2, e=2),
             )
-            h_turn = psum.tile([P, 2, SLOTS], F32, tag="h_turn")
+            h_turn = banks.tile([P, 2, SLOTS], F32, tag="bank%d" % (6 + m % 2), name="h_turn")
             pairs = h_bf[:].bitcast(F32)
             for u in range(2):
                 nc.tensor.transpose(h_turn[:, u, :], pairs[:, u * P:(u + 1) * P], ident[:])
@@ -174,7 +172,7 @@ def tile_moe_dyl_none_kernel(
         def second_layer(m):
             sc = slice((m % 2) * N, (m % 2 + 1) * N)
             hc = slice((m % 2) * SLOTS, (m % 2 + 1) * SLOTS)
-            y_acc = psum.tile([P, N], F32, tag="y_acc")
+            y_acc = banks.tile([P, N], F32, tag="bank%d" % (m % 2), name="y_acc")
             nc.tensor.matmul_mx(
                 out=y_acc[:], lhsT=hq[m // 2][:, hc].bitcast(FP8X4), lhsT_scale=hqs[m // 2][:, hc],
                 rhs=bg[:, m * N:(m + 1) * N].bitcast(FP8X4), rhs_scale=bsg[m // 2][B_ROW:, sc], start=True, stop=True,
@@ -184,7 +182,7 @@ def tile_moe_dyl_none_kernel(
                 out=y_sb[:], in_=y_acc[:].rearrange("s (p t) -> s t p", t=PACK), func=COPY,
                 scale=gate_col[:, m:m + 1],
             )
-            y_turn = psum.tile([P, PACK, SLOTS], F32, tag="y_turn")
+            y_turn = banks.tile([P, PACK, SLOTS], F32, tag="bank%d" % (2 + m % 2), name="y_turn")
             for t in range(PACK):
                 nc.tensor.transpose(y_turn[:, t, :], y_sb[:, t, :], ident[:])
             nc.scalar.copy(out=gated[:, :, m * SLOTS:(m + 1) * SLOTS], in_=y_turn[:])
@@ -200,6 +198,8 @@ def tile_moe_dyl_none_kernel(
             gather(nc, bg[:, cols].bitcast(U32), b_win[:].bitcast(U32), b_list, q * 2 * N, 2 * N)
             second_layer(2 * q)
             second_layer(2 * q + 1)
+            if q == 0:
+                frozen_rest()
 
         result = [keep.tile([P, WINDOW], F32, align_bytes=64, name="result%d" % t) for t in range(PACK)]
 
@@ -211,26 +211,34 @@ def tile_moe_dyl_none_kernel(
 
         for t in range(PACK):
             scatter(t, 0, 256)
-        for t in range(PACK):
+        for t in range(2):
+            scatter(t, 256, 512)
+        for t in range(2):
+            scatter(t, 512, T)
+        for t in range(2, PACK):
             scatter(t, 256, T)
 
+        last = PACK - 1
         C = T // 3
         woven = [keep.tile([P, C, PACK], BF16, align_bytes=64, name="woven%d" % c) for c in range(3)]
+        planes = keep.tile([P, PACK, C], BF16, align_bytes=64)
         out_rows = out_0.rearrange("(p t) c -> p t c", t=PACK)
         for t in range(PACK):
             nc.sync.dma_start(out=out_rows[:, t, :], in_=result[t][:, :T])
-            for c in range(3):
-                values = result[t][:, c * C:(c + 1) * C]
-                if c > 0 and t == 2:
-                    nc.scalar.copy(out=woven[c][:, :, 2:4], in_=values.unsqueeze(2).to_broadcast([P, C, 2]))
-                elif c > 0 and t == 3:
-                    nc.vector.tensor_copy(out=woven[c][:, :, t], in_=values)
-                else:
-                    nc.scalar.copy(out=woven[c][:, :, t], in_=values)
+            for c in range(2):
+                nc.scalar.copy(out=woven[c][:, :, t], in_=result[t][:, c * C:(c + 1) * C])
+            if t == last:
+                nc.vector.tensor_copy(out=planes[:, t, :], in_=result[t][:, 2 * C:T])
+            else:
+                nc.scalar.copy(out=planes[:, t, :], in_=result[t][:, 2 * C:T])
+        nc.vector.tensor_copy(
+            out=woven[2][:].rearrange("p (c i) t -> p c t i", i=4),
+            in_=planes[:].rearrange("p t (c i) -> p c t i", i=4),
+        )
 
         out_scales = keep.tile([P, T], U8, align_bytes=64)
         out_words = out_1[0].rearrange("p c d -> p (c d)").bitcast(I32)
-        for c in (1, 0, 2):
+        for c in (0, 2, 1):
             codes = keep.tile([P, C], I32, align_bytes=64, name="codes%d" % c)
             nc.vector.quantize_mx(
                 out=codes[:].bitcast(FP8X4), scales=out_scales[:, c * C:(c + 1) * C],

@@ -55,15 +55,15 @@ def tile_moe_dyl_none_kernel(
         tok_list = keep.tile([P, T // PER_COL], U16)
         a_list = keep.tile([P, B * H // PER_COL], U16)
         b_list = keep.tile([P, B * N // PER_COL], U16)
-        x_win = keep.tile([P, WINDOW], I32, align_bytes=64, tag="x_then_a")
-        xs_win = keep.tile([P, WINDOW], U8, align_bytes=64)
+        x_win = keep.tile([P, WINDOW], I32, align_bytes=64)
+        xs_win = keep.tile([P, WINDOW], U8, align_bytes=64, tag="xs_then_a")
         as_win = keep.tile([P, E * H], U8, align_bytes=64)
         bs_win = keep.tile([P, E * N], U8, align_bytes=64)
         w_raw = shared.tile([P, PACK, N], F32, align_bytes=64, offset=11 * 1024)
         ident = keep.tile([P, P], F32, align_bytes=64)
 
-        nc.vector.memset(as_win[:].bitcast(I32), 0)
         nc.vector.memset(xs_win[:].bitcast(I32), 0)
+        nc.vector.memset(as_win[:].bitcast(I32), 0)
         nc.gpsimd.memset(x_win[:, T:], 0)
         nc.vector.memset(bs_win[:].bitcast(I32), 0)
         make_identity(nc, ident[:])
@@ -73,15 +73,16 @@ def tile_moe_dyl_none_kernel(
         nc.sync.dma_start(a_list[:], offs2)
         nc.sync.dma_start(b_list[:], offs3)
         nc.sync.dma_start(out=w_raw[:], in_=w.rearrange("(p j) n -> p j n", j=PACK))
+        load_scale_rows(nc.scalar, xs_win[:, :T], x_scales, 0)
         load_scale_rows(nc.scalar, as_win[:], wa_scales, A_ROW)
-        load_scale_rows(nc.sync, xs_win[:, :T], x_scales, 0)
-        load_scale_rows(nc.scalar, bs_win[:], wb_scales, B_ROW)
+        load_scale_rows(nc.sync, bs_win[:], wb_scales, B_ROW)
 
         xg = keep.tile([P, T], I32, align_bytes=64)
         xsg = keep.tile([P, T], U8, align_bytes=64)
-        gather(nc, xg[:].bitcast(U32), x_win[:].bitcast(U32), tok_list, 0, T)
-        a_win = keep.tile([P, E * H], I32, align_bytes=64, tag="x_then_a")
+        gather(nc, xsg[:], xs_win[:], tok_list, 0, T)
+        a_win = keep.tile([P, E * H], I32, align_bytes=64, tag="xs_then_a")
         load_words(nc.sync, a_win[:], wa_words)
+        gather(nc, xg[:].bitcast(U32), x_win[:].bitcast(U32), tok_list, 0, T)
 
         asg = []
 
@@ -91,7 +92,6 @@ def tile_moe_dyl_none_kernel(
 
         for q in range(2):
             gather_a_scales(q, keep.tile([P, 2 * H], U8, align_bytes=64, name="asg%d" % q, tag="scales%d" % q))
-        gather(nc, xsg[:], xs_win[:], tok_list, 0, T)
 
         w_bf = keep.tile([P, N * PACK], BF16, align_bytes=64, tag="wbf_then_gate")
         nc.scalar.copy(
@@ -211,34 +211,33 @@ def tile_moe_dyl_none_kernel(
 
         for t in range(PACK):
             scatter(t, 0, 256)
-        for t in range(2):
+        finish = (2, 0, 1, 3)
+        for t in finish[:2]:
             scatter(t, 256, 512)
-        for t in range(2):
+        for t in finish[:2]:
             scatter(t, 512, T)
-        for t in range(2, PACK):
+        for t in finish[2:]:
             scatter(t, 256, T)
 
-        last = PACK - 1
         C = T // 3
         woven = [keep.tile([P, C, PACK], BF16, align_bytes=64, name="woven%d" % c) for c in range(3)]
-        planes = keep.tile([P, PACK, C], BF16, align_bytes=64)
         out_rows = out_0.rearrange("(p t) c -> p t c", t=PACK)
-        for t in range(PACK):
+        for t in finish:
             nc.sync.dma_start(out=out_rows[:, t, :], in_=result[t][:, :T])
-            for c in range(2):
-                nc.scalar.copy(out=woven[c][:, :, t], in_=result[t][:, c * C:(c + 1) * C])
-            if t == last:
-                nc.vector.tensor_copy(out=planes[:, t, :], in_=result[t][:, 2 * C:T])
-            else:
-                nc.scalar.copy(out=planes[:, t, :], in_=result[t][:, 2 * C:T])
-        nc.vector.tensor_copy(
-            out=woven[2][:].rearrange("p (c i) t -> p c t i", i=4),
-            in_=planes[:].rearrange("p t (c i) -> p c t i", i=4),
-        )
+            for c, c0, c1, on_vector in ((0, 0, C, True), (2, 0, C // 2, True), (1, 0, C, False), (2, C // 2, C, False)):
+                values = result[t][:, c * C + c0:c * C + c1]
+                if on_vector and t == 2:
+                    nc.scalar.copy(
+                        out=woven[c][:, c0:c1, 2:4], in_=values.unsqueeze(2).to_broadcast([P, c1 - c0, 2]),
+                    )
+                elif on_vector and t == 3:
+                    nc.vector.tensor_copy(out=woven[c][:, c0:c1, t], in_=values)
+                else:
+                    nc.scalar.copy(out=woven[c][:, c0:c1, t], in_=values)
 
         out_scales = keep.tile([P, T], U8, align_bytes=64)
         out_words = out_1[0].rearrange("p c d -> p (c d)").bitcast(I32)
-        for c in (0, 2, 1):
+        for c in range(3):
             codes = keep.tile([P, C], I32, align_bytes=64, name="codes%d" % c)
             nc.vector.quantize_mx(
                 out=codes[:].bitcast(FP8X4), scales=out_scales[:, c * C:(c + 1) * C],

@@ -55,34 +55,40 @@ def tile_moe_dyl_none_kernel(
         tok_list = keep.tile([P, T // PER_COL], U16)
         a_list = keep.tile([P, B * H // PER_COL], U16)
         b_list = keep.tile([P, B * N // PER_COL], U16)
-        x_win = keep.tile([P, WINDOW], I32, align_bytes=64)
-        xs_win = keep.tile([P, WINDOW], U8, align_bytes=64, tag="xs_then_a")
+        x_win = keep.tile([P, WINDOW], I32, align_bytes=64, tag="x_then_a")
+        xs_win = keep.tile([P, WINDOW], U8, align_bytes=64)
         as_win = keep.tile([P, E * H], U8, align_bytes=64)
         bs_win = keep.tile([P, E * N], U8, align_bytes=64)
-        w_raw = shared.tile([P, PACK, N], F32, align_bytes=64, offset=11 * 1024)
+        w_raw = [
+            shared.tile([P, PACK, N // 2], F32, align_bytes=64, name="w_raw%d" % i, offset=(15 - 4 * i) * 1024)
+            for i in range(2)
+        ]
         ident = keep.tile([P, P], F32, align_bytes=64)
 
         nc.vector.memset(xs_win[:].bitcast(I32), 0)
-        nc.vector.memset(as_win[:].bitcast(I32), 0)
+        nc.gpsimd.memset(as_win[:, :E * H // 2].bitcast(I32), 0)
+        nc.vector.memset(as_win[:, E * H // 2:].bitcast(I32), 0)
         nc.gpsimd.memset(x_win[:, T:], 0)
         nc.vector.memset(bs_win[:].bitcast(I32), 0)
         make_identity(nc, ident[:])
 
         nc.sync.dma_start(tok_list[:], offs)
         load_words(nc.sync, x_win[:, :T], x_words)
+        load_scale_rows(nc.sync, xs_win[:, :T], x_scales, 0)
+        load_scale_rows(nc.sync, as_win[:], wa_scales, A_ROW)
         nc.sync.dma_start(a_list[:], offs2)
+        w_rows = w.rearrange("(p j) n -> p j n", j=PACK)
+        for i in range(2):
+            nc.sync.dma_start(out=w_raw[i][:], in_=w_rows[:, :, i * N // 2:(i + 1) * N // 2])
         nc.sync.dma_start(b_list[:], offs3)
-        nc.sync.dma_start(out=w_raw[:], in_=w.rearrange("(p j) n -> p j n", j=PACK))
-        load_scale_rows(nc.scalar, xs_win[:, :T], x_scales, 0)
-        load_scale_rows(nc.scalar, as_win[:], wa_scales, A_ROW)
         load_scale_rows(nc.sync, bs_win[:], wb_scales, B_ROW)
 
         xg = keep.tile([P, T], I32, align_bytes=64)
         xsg = keep.tile([P, T], U8, align_bytes=64)
-        gather(nc, xsg[:], xs_win[:], tok_list, 0, T)
-        a_win = keep.tile([P, E * H], I32, align_bytes=64, tag="xs_then_a")
-        load_words(nc.sync, a_win[:], wa_words)
         gather(nc, xg[:].bitcast(U32), x_win[:].bitcast(U32), tok_list, 0, T)
+        a_win = keep.tile([P, E * H], I32, align_bytes=64, tag="x_then_a")
+        load_words(nc.sync, a_win[:], wa_words)
+        gather(nc, xsg[:], xs_win[:], tok_list, 0, T)
 
         asg = []
 
@@ -94,10 +100,11 @@ def tile_moe_dyl_none_kernel(
             gather_a_scales(q, keep.tile([P, 2 * H], U8, align_bytes=64, name="asg%d" % q, tag="scales%d" % q))
 
         w_bf = keep.tile([P, N * PACK], BF16, align_bytes=64, tag="wbf_then_gate")
-        nc.scalar.copy(
-            out=w_bf[:].rearrange("p (t m j) -> p m t j", t=PACK, j=PACK),
-            in_=w_raw[:].rearrange("p j (m t) -> p m t j", t=PACK),
-        )
+        for i in range(2):
+            nc.scalar.copy(
+                out=w_bf[:].rearrange("p (t m j) -> p m t j", t=PACK, j=PACK)[:, i * P // 2:(i + 1) * P // 2],
+                in_=w_raw[i][:].rearrange("p j (m t) -> p m t j", t=PACK),
+            )
         wq = keep.tile([P, N], I32, align_bytes=64)
         wqs = keep.tile([P, N], U8, align_bytes=64)
         nc.vector.quantize_mx(out=wq[:].bitcast(FP8X4), scales=wqs[:], in_=w_bf[:])

@@ -19,7 +19,9 @@ ADD = mybir.AluOpType.add
 P = 128
 PACK = 4
 SLOTS = 128
+PAIR = 2 * SLOTS
 PAIRS = B // 2
+TURNED_PLANES = (1, 2, 2)
 PER_COL = 16
 WINDOW = 1024
 A_ROW, B_ROW = 4, 8
@@ -115,26 +117,45 @@ def tile_moe_dyl_none_kernel(
             nc.sync.dma_start(out=gate_col[:], in_=gate[0:1, :].rearrange("o (m u) -> u (o m)", u=SLOTS))
         gather_a_scales(2, shared.tile([P, 2 * H], U8, align_bytes=64, name="asg2", offset=12 * 1024))
 
-        base = keep.tile([P, PACK, T], F32, align_bytes=64)
+        def frozen_by_slot(acc, m, planes):
+            block = slice(m * SLOTS, (m + 1) * SLOTS)
+            nc.tensor.matmul_mx(
+                out=acc, lhsT=xg[:, block].bitcast(FP8X4), lhsT_scale=xsg[:, block],
+                rhs=wq[:, :planes * P].bitcast(FP8X4), rhs_scale=wqs[:, :planes * P], start=True, stop=True,
+            )
 
-        def frozen(acc, t, s0, s1):
+        def frozen_by_plane(acc, t, s0, s1):
             cols = slice(t * P, (t + 1) * P)
             nc.tensor.matmul_mx(
                 out=acc, lhsT=wq[:, cols].bitcast(FP8X4), lhsT_scale=wqs[:, cols],
                 rhs=xg[:, s0:s1].bitcast(FP8X4), rhs_scale=xsg[:, s0:s1], start=True, stop=True,
             )
 
-        for t in range(PACK):
-            acc = banks.tile([P, 512], F32, tag="bank%d" % t, name="base_acc")
-            frozen(acc[:], t, 0, 512)
-            nc.scalar.copy(out=base[:, t, 0:512], in_=acc[:])
+        base_slot = [keep.tile([P, 2 * PAIR], F32, align_bytes=64, name="base_slot%d" % q) for q in range(PAIRS)]
+        base_high = keep.tile([P, 2, T], F32, align_bytes=64)
+
+        def frozen_slots(q, bank):
+            width = TURNED_PLANES[q] * P
+            acc = banks.tile([P, 2 * PAIR], F32, tag="bank%d" % bank, name="slot_acc")
+            for i in range(2):
+                frozen_by_slot(acc[:, i * width:(i + 1) * width], 2 * q + i, TURNED_PLANES[q])
+            if q == 0:
+                frozen_by_plane(acc[:, PAIR:], 1, 0, PAIR)
+            nc.scalar.copy(out=base_slot[q][:], in_=acc[:])
+
+        frozen_slots(0, 0)
+        frozen_slots(1, 1)
+        for u in range(2):
+            acc = banks.tile([P, 2 * PAIR], F32, tag="bank%d" % (2 + u), name="high_acc")
+            frozen_by_plane(acc[:], 2 + u, 0, 2 * PAIR)
+            nc.scalar.copy(out=base_high[:, u, :2 * PAIR], in_=acc[:])
 
         def frozen_rest():
-            for t in range(0, PACK, 2):
-                acc = banks.tile([P, 2, T - 512], F32, tag="bank%d" % (t // 2), name="rest_acc")
-                for u in range(2):
-                    frozen(acc[:, u, :], t + u, 512, T)
-                nc.scalar.copy(out=base[:, t:t + 2, 512:T], in_=acc[:])
+            frozen_slots(2, 0)
+            acc = banks.tile([P, 2, PAIR], F32, tag="bank1", name="rest_acc")
+            for u in range(2):
+                frozen_by_plane(acc[:, u, :], 2 + u, 2 * PAIR, T)
+            nc.scalar.copy(out=base_high[:, :, 2 * PAIR:], in_=acc[:])
 
         ag = shared.tile([P, B * H], I32, align_bytes=64, offset=0)
         bg = keep.tile([P, B * N], I32, align_bytes=64)
@@ -190,8 +211,15 @@ def tile_moe_dyl_none_kernel(
                 scale=gate_col[:, m:m + 1],
             )
             y_turn = banks.tile([P, PACK, SLOTS], F32, tag="bank%d" % (2 + m % 2), name="y_turn")
-            for t in range(PACK):
-                nc.tensor.transpose(y_turn[:, t, :], y_sb[:, t, :], ident[:])
+            planes = TURNED_PLANES[m // 2]
+            first = (m % 2) * planes
+            terms = [(t, base_slot[m // 2][:, (first + t) * P:(first + t + 1) * P]) for t in range(planes)]
+            terms = terms + [(t, y_sb[:, t, :]) for t in range(PACK)]
+            for k, (t, term) in enumerate(terms):
+                nc.tensor.matmul(
+                    y_turn[:, t, :], lhsT=term, rhs=ident[:], is_transpose=True,
+                    start=(k == 0), stop=(k == len(terms) - 1),
+                )
             nc.scalar.copy(out=gated[:, :, m * SLOTS:(m + 1) * SLOTS], in_=y_turn[:])
 
         for q in range(PAIRS):
@@ -199,51 +227,58 @@ def tile_moe_dyl_none_kernel(
             gather(nc, ag[:, cols].bitcast(U32), a_win[:].bitcast(U32), a_list, q * 2 * H, 2 * H)
         for q in range(PAIRS):
             first_pair(q)
+        frozen_rest()
+
+        result = [keep.tile([P, WINDOW], F32, align_bytes=64, name="result%d" % t) for t in range(PACK)]
+
+        def window(t, s0, s1):
+            return result[t][:].indirect(tok_list[:, s0 // PER_COL:s1 // PER_COL])
+
+        def scatter_sum(t, s0, s1):
+            nc.scalar.activation(window(t, s0, s1), gated[:, t, s0:s1], COPY)
+
+        def scatter_add(t, s0, s1, base):
+            nc.vector.tensor_tensor(window(t, s0, s1), gated[:, t, s0:s1], base, ADD)
+
         for q in range(PAIRS):
             cols = slice(q * 2 * N, (q + 1) * 2 * N)
             gather_b_scales(q)
             gather(nc, bg[:, cols].bitcast(U32), b_win[:].bitcast(U32), b_list, q * 2 * N, 2 * N)
             second_layer(2 * q)
             second_layer(2 * q + 1)
-            if q == 0:
-                frozen_rest()
+            if q < PAIRS - 1:
+                scatter_sum(0, q * PAIR + SLOTS, (q + 1) * PAIR)
 
-        result = [keep.tile([P, WINDOW], F32, align_bytes=64, name="result%d" % t) for t in range(PACK)]
+        scatter_add(1, 0, PAIR, base_slot[0][:, PAIR:])
+        for q in range(PAIRS):
+            for t in (3, 2):
+                scatter_add(t, q * PAIR, (q + 1) * PAIR, base_high[:, t - 2, q * PAIR:(q + 1) * PAIR])
+        scatter_sum(0, 2 * PAIR, T)
+        scatter_sum(0, 0, SLOTS)
+        scatter_sum(0, PAIR, PAIR + SLOTS)
+        scatter_sum(1, 2 * PAIR, T)
+        scatter_sum(1, PAIR, 2 * PAIR)
 
-        def scatter(t, s0, s1):
-            nc.vector.tensor_tensor(
-                result[t][:].indirect(tok_list[:, s0 // PER_COL:s1 // PER_COL]),
-                gated[:, t, s0:s1], base[:, t, s0:s1], ADD,
-            )
-
-        for t in range(PACK):
-            scatter(t, 0, 256)
-        finish = (2, 0, 1, 3)
-        for t in finish[:2]:
-            scatter(t, 256, 512)
-        for t in finish[:2]:
-            scatter(t, 512, T)
-        for t in finish[2:]:
-            scatter(t, 256, T)
+        planes = keep.tile([P, PACK, T], BF16, align_bytes=64)
+        out_rows = out_0.rearrange("(p t) c -> p t c", t=PACK)
+        for t in (0, 3, 1, 2):
+            nc.sync.dma_start(out=out_rows[:, t, :], in_=result[t][:, :T])
+            if t >= 2:
+                nc.vector.tensor_copy(out=planes[:, t, :], in_=result[t][:, :T])
+            else:
+                nc.scalar.copy(out=planes[:, t, :], in_=result[t][:, :T])
 
         C = T // 3
-        woven = [keep.tile([P, C, PACK], BF16, align_bytes=64, name="woven%d" % c) for c in range(3)]
-        out_rows = out_0.rearrange("(p t) c -> p t c", t=PACK)
-        for t in finish:
-            nc.sync.dma_start(out=out_rows[:, t, :], in_=result[t][:, :T])
-            for c, c0, c1, on_vector in ((0, 0, C, True), (2, 0, C // 2, True), (1, 0, C, False), (2, C // 2, C, False)):
-                values = result[t][:, c * C + c0:c * C + c1]
-                if on_vector and t == 2:
-                    nc.scalar.copy(
-                        out=woven[c][:, c0:c1, 2:4], in_=values.unsqueeze(2).to_broadcast([P, c1 - c0, 2]),
-                    )
-                elif on_vector and t == 3:
-                    nc.vector.tensor_copy(out=woven[c][:, c0:c1, t], in_=values)
-                else:
-                    nc.scalar.copy(out=woven[c][:, c0:c1, t], in_=values)
-
         out_scales = keep.tile([P, T], U8, align_bytes=64)
         out_words = out_1[0].rearrange("p c d -> p (c d)").bitcast(I32)
+        woven = [keep.tile([P, C, PACK], BF16, align_bytes=64, name="woven%d" % c) for c in range(3)]
+        for c in range(3):
+            src = planes[:, :, c * C:(c + 1) * C].rearrange("p t (c i) -> p c t i", i=4)
+            dst = woven[c][:].rearrange("p (c i) t -> p c t i", i=4)
+            if c == 2:
+                nc.scalar.copy(out=dst, in_=src)
+            else:
+                nc.vector.tensor_copy(out=dst, in_=src)
         for c in range(3):
             codes = keep.tile([P, C], I32, align_bytes=64, name="codes%d" % c)
             nc.vector.quantize_mx(

@@ -21,7 +21,7 @@ PACK = 4
 SLOTS = 128
 PAIR = 2 * SLOTS
 PAIRS = B // 2
-TURNED_PLANES = (1, 2, 2)
+KIB = 1024
 PER_COL = 16
 WINDOW = 1024
 A_ROW, B_ROW = 4, 8
@@ -117,153 +117,186 @@ def tile_moe_dyl_none_kernel(
             nc.sync.dma_start(out=gate_col[:], in_=gate[0:1, :].rearrange("o (m u) -> u (o m)", u=SLOTS))
         gather_a_scales(2, shared.tile([P, 2 * H], U8, align_bytes=64, name="asg2", offset=12 * 1024))
 
-        def frozen_by_slot(acc, m, planes):
-            block = slice(m * SLOTS, (m + 1) * SLOTS)
-            nc.tensor.matmul_mx(
-                out=acc, lhsT=xg[:, block].bitcast(FP8X4), lhsT_scale=xsg[:, block],
-                rhs=wq[:, :planes * P].bitcast(FP8X4), rhs_scale=wqs[:, :planes * P], start=True, stop=True,
-            )
+        def placed(name, shape, dtype, offset):
+            return shared.tile(shape, dtype, align_bytes=64, name=name, offset=offset)
 
-        def frozen_by_plane(acc, t, s0, s1):
+        def bank(number, shape, name):
+            return banks.tile(shape, F32, tag="bank%d" % number, name=name)
+
+        base_low = [keep.tile([P, 2, PAIR], F32, align_bytes=64, name="base_low%d" % q) for q in range(PAIRS)]
+        base_high = keep.tile([P, 2, T], F32, align_bytes=64)
+
+        def frozen_low(q, number):
+            acc = bank(number, [P, 2, PAIR], "low_acc")
+            for i in range(2):
+                block = slice((2 * q + i) * SLOTS, (2 * q + i + 1) * SLOTS)
+                nc.tensor.matmul_mx(
+                    out=acc[:, i, :], lhsT=xg[:, block].bitcast(FP8X4), lhsT_scale=xsg[:, block],
+                    rhs=wq[:, :2 * P].bitcast(FP8X4), rhs_scale=wqs[:, :2 * P], start=True, stop=True,
+                )
+            nc.scalar.copy(out=base_low[q][:], in_=acc[:])
+
+        def frozen_high(acc, t, s0, s1):
             cols = slice(t * P, (t + 1) * P)
             nc.tensor.matmul_mx(
                 out=acc, lhsT=wq[:, cols].bitcast(FP8X4), lhsT_scale=wqs[:, cols],
                 rhs=xg[:, s0:s1].bitcast(FP8X4), rhs_scale=xsg[:, s0:s1], start=True, stop=True,
             )
 
-        base_slot = [keep.tile([P, 2 * PAIR], F32, align_bytes=64, name="base_slot%d" % q) for q in range(PAIRS)]
-        base_high = keep.tile([P, 2, T], F32, align_bytes=64)
-
-        def frozen_slots(q, bank):
-            width = TURNED_PLANES[q] * P
-            acc = banks.tile([P, 2 * PAIR], F32, tag="bank%d" % bank, name="slot_acc")
-            for i in range(2):
-                frozen_by_slot(acc[:, i * width:(i + 1) * width], 2 * q + i, TURNED_PLANES[q])
-            if q == 0:
-                frozen_by_plane(acc[:, PAIR:], 1, 0, PAIR)
-            nc.scalar.copy(out=base_slot[q][:], in_=acc[:])
-
-        frozen_slots(0, 0)
-        frozen_slots(1, 1)
+        for q in range(2):
+            frozen_low(q, q)
         for u in range(2):
-            acc = banks.tile([P, 2 * PAIR], F32, tag="bank%d" % (2 + u), name="high_acc")
-            frozen_by_plane(acc[:], 2 + u, 0, 2 * PAIR)
+            acc = bank(2 + u, [P, 2 * PAIR], "high_acc")
+            frozen_high(acc[:], 2 + u, 0, 2 * PAIR)
             nc.scalar.copy(out=base_high[:, u, :2 * PAIR], in_=acc[:])
 
-        def frozen_rest():
-            frozen_slots(2, 0)
-            acc = banks.tile([P, 2, PAIR], F32, tag="bank1", name="rest_acc")
-            for u in range(2):
-                frozen_by_plane(acc[:, u, :], 2 + u, 2 * PAIR, T)
-            nc.scalar.copy(out=base_high[:, :, 2 * PAIR:], in_=acc[:])
-
         ag = shared.tile([P, B * H], I32, align_bytes=64, offset=0)
-        bg = keep.tile([P, B * N], I32, align_bytes=64)
-        hq = [keep.tile([P, 2 * SLOTS], I32, align_bytes=64, name="hq%d" % q) for q in range(PAIRS)]
-        hqs = [keep.tile([P, 2 * SLOTS], U8, align_bytes=64, name="hqs%d" % q) for q in range(PAIRS)]
-        gated = keep.tile([P, PACK, T], F32, align_bytes=64)
-        bsg = []
-
-        def first_layer(m, h_grp):
-            slots = slice(m * SLOTS, (m + 1) * SLOTS)
-            sc = slice((m % 2) * H, (m % 2 + 1) * H)
-            h_acc = banks.tile([P, H], F32, tag="bank%d" % (4 + m % 2), name="h_acc")
-            nc.tensor.matmul_mx(
-                out=h_acc[:], lhsT=xg[:, slots].bitcast(FP8X4), lhsT_scale=xsg[:, slots],
-                rhs=ag[:, m * H:(m + 1) * H].bitcast(FP8X4), rhs_scale=asg[m // 2][A_ROW:, sc], start=True, stop=True,
-            )
-            h_bf = ring.tile([P, H], BF16, align_bytes=64)
-            nc.scalar.copy(
-                out=h_bf[:].rearrange("s (u p e) -> s u p e", u=2, e=2),
-                in_=h_acc[:].rearrange("s (p u e) -> s u p e", u=2, e=2),
-            )
-            h_turn = banks.tile([P, 2, SLOTS], F32, tag="bank%d" % (6 + m % 2), name="h_turn")
-            pairs = h_bf[:].bitcast(F32)
-            for u in range(2):
-                nc.tensor.transpose(h_turn[:, u, :], pairs[:, u * P:(u + 1) * P], ident[:])
-            nc.scalar.copy(
-                out=h_grp.bitcast(F32).rearrange("p (s u) -> p s u", u=2),
-                in_=h_turn[:].rearrange("p u s -> p s u"),
-            )
-
-        def first_pair(q):
-            width = SLOTS * PACK
-            h_grp = keep.tile([P, 2 * width], BF16, align_bytes=64, name="h_grp%d" % q)
-            for i in range(2):
-                first_layer(2 * q + i, h_grp[:, i * width:(i + 1) * width])
-            nc.vector.quantize_mx(out=hq[q][:].bitcast(FP8X4), scales=hqs[q][:], in_=h_grp[:])
-
-        def gather_b_scales(q):
-            bsg.append(keep.tile([P, 2 * N], U8, align_bytes=64, name="bsg%d" % q, tag="scales%d" % (q % 2)))
-            gather(nc, bsg[q][:], bs_win[:], b_list, q * 2 * N, 2 * N)
-
-        def second_layer(m):
-            sc = slice((m % 2) * N, (m % 2 + 1) * N)
-            hc = slice((m % 2) * SLOTS, (m % 2 + 1) * SLOTS)
-            y_acc = banks.tile([P, N], F32, tag="bank%d" % (m % 2), name="y_acc")
-            nc.tensor.matmul_mx(
-                out=y_acc[:], lhsT=hq[m // 2][:, hc].bitcast(FP8X4), lhsT_scale=hqs[m // 2][:, hc],
-                rhs=bg[:, m * N:(m + 1) * N].bitcast(FP8X4), rhs_scale=bsg[m // 2][B_ROW:, sc], start=True, stop=True,
-            )
-            y_sb = ring.tile([P, PACK, P], F32, align_bytes=64)
-            nc.scalar.activation(
-                out=y_sb[:], in_=y_acc[:].rearrange("s (p t) -> s t p", t=PACK), func=COPY,
-                scale=gate_col[:, m:m + 1],
-            )
-            y_turn = banks.tile([P, PACK, SLOTS], F32, tag="bank%d" % (2 + m % 2), name="y_turn")
-            planes = TURNED_PLANES[m // 2]
-            first = (m % 2) * planes
-            terms = [(t, base_slot[m // 2][:, (first + t) * P:(first + t + 1) * P]) for t in range(planes)]
-            terms = terms + [(t, y_sb[:, t, :]) for t in range(PACK)]
-            for k, (t, term) in enumerate(terms):
-                nc.tensor.matmul(
-                    y_turn[:, t, :], lhsT=term, rhs=ident[:], is_transpose=True,
-                    start=(k == 0), stop=(k == len(terms) - 1),
-                )
-            nc.scalar.copy(out=gated[:, :, m * SLOTS:(m + 1) * SLOTS], in_=y_turn[:])
-
         for q in range(PAIRS):
             cols = slice(q * 2 * H, (q + 1) * 2 * H)
             gather(nc, ag[:, cols].bitcast(U32), a_win[:].bitcast(U32), a_list, q * 2 * H, 2 * H)
-        for q in range(PAIRS):
-            first_pair(q)
-        frozen_rest()
+
+        h_grp = [placed("h_grp%d" % q, [P, 2 * H], BF16, (40 + 16 * q) * KIB) for q in range(2)]
+        h_bf = []
+
+        def h_rounded(m, number):
+            slots = slice(m * SLOTS, (m + 1) * SLOTS)
+            sc = slice((m % 2) * H, (m % 2 + 1) * H)
+            acc = bank(number, [P, H], "h_acc")
+            nc.tensor.matmul_mx(
+                out=acc[:], lhsT=xg[:, slots].bitcast(FP8X4), lhsT_scale=xsg[:, slots],
+                rhs=ag[:, m * H:(m + 1) * H].bitcast(FP8X4), rhs_scale=asg[m // 2][A_ROW:, sc], start=True, stop=True,
+            )
+            h_bf.append(keep.tile([P, H], BF16, align_bytes=64, name="h_bf%d" % m))
+            nc.scalar.copy(
+                out=h_bf[m][:].rearrange("s (u p e) -> s u p e", u=2, e=2),
+                in_=acc[:].rearrange("s (p u e) -> s u p e", u=2, e=2),
+            )
+
+        def h_turned(q, number, copy):
+            turn = bank(number, [P, 2, 2, SLOTS], "h_turn")
+            for i in range(2):
+                pairs = h_bf[2 * q + i][:].bitcast(F32)
+                for u in range(2):
+                    nc.tensor.transpose(turn[:, i, u, :], pairs[:, u * P:(u + 1) * P], ident[:])
+            copy(
+                out=h_grp[q][:].bitcast(F32).rearrange("p (i s u) -> p i s u", i=2, u=2),
+                in_=turn[:].rearrange("p i u s -> p i s u"),
+            )
+
+        for m, number in enumerate((6, 7, 0, 1, 6)):
+            h_rounded(m, number)
+        h_turned(0, 2, nc.scalar.copy)
+        h_rounded(5, 7)
+        h_turned(1, 3, nc.scalar.copy)
+        frozen_low(2, 0)
+        acc = bank(1, [P, 2, PAIR], "rest_acc")
+        for u in range(2):
+            frozen_high(acc[:, u, :], 2 + u, 2 * PAIR, T)
+        nc.scalar.copy(out=base_high[:, :, 2 * PAIR:], in_=acc[:])
+
+        bsg = []
+        hq = []
+
+        def b_scales(q, tile):
+            gather(nc, tile[:], bs_win[:], b_list, q * 2 * N, 2 * N)
+            bsg.append(tile)
+
+        def b_words(out, m, blocks):
+            gather(nc, out.bitcast(U32), b_win[:].bitcast(U32), b_list, m * N, blocks * N)
+
+        def quantize_h(q, codes):
+            scales = keep.tile([P, PAIR], U8, align_bytes=64, name="hqs%d" % q)
+            nc.vector.quantize_mx(out=codes[:].bitcast(FP8X4), scales=scales[:], in_=h_grp[q][:])
+            hq.append((codes, scales))
+
+        for q in range(2):
+            b_scales(q, keep.tile([P, 2 * N], U8, align_bytes=64, name="bsg%d" % q, tag="scales%d" % q))
+        quantize_h(0, keep.tile([P, PAIR], I32, align_bytes=64, name="hq0"))
+        bg0 = placed("bg0", [P, N], I32, 38 * KIB + 512)
+        b_words(bg0[:], 0, 1)
+        bg_mid = placed("bg_mid", [P, 3 * N], I32, 41 * KIB)
+        b_words(bg_mid[:, :N], 1, 1)
+        b_words(bg_mid[:, N:], 2, 2)
+        words = [bg0[:]] + [bg_mid[:, i * N:(i + 1) * N] for i in range(3)]
+
+        summed = keep.tile([P, PACK, T], F32, align_bytes=64)
+
+        def y_gated(m, number):
+            sc = slice((m % 2) * N, (m % 2 + 1) * N)
+            hc = slice((m % 2) * SLOTS, (m % 2 + 1) * SLOTS)
+            acc = bank(number, [P, N], "y_acc")
+            nc.tensor.matmul_mx(
+                out=acc[:], lhsT=hq[m // 2][0][:, hc].bitcast(FP8X4), lhsT_scale=hq[m // 2][1][:, hc],
+                rhs=words[m].bitcast(FP8X4), rhs_scale=bsg[m // 2][B_ROW:, sc], start=True, stop=True,
+            )
+            y_sb = ring.tile([P, PACK, P], F32, align_bytes=64, bufs=4)
+            nc.scalar.activation(
+                out=y_sb[:], in_=acc[:].rearrange("s (p t) -> s t p", t=PACK), func=COPY,
+                scale=gate_col[:, m:m + 1],
+            )
+            return y_sb
+
+        def y_turned(m, y_sb, number, frozen_first):
+            turn = bank(number, [P, PACK, SLOTS], "y_turn")
+            frozen = [(t, base_low[m // 2][:, m % 2, t * P:(t + 1) * P]) for t in range(2)]
+            adapter = [(t, y_sb[:, t, :]) for t in range(PACK)]
+            terms = frozen + adapter if frozen_first else adapter + frozen
+            for k, (t, term) in enumerate(terms):
+                nc.tensor.matmul(
+                    turn[:, t, :], lhsT=term, rhs=ident[:], is_transpose=True,
+                    start=(k == 0), stop=(k == len(terms) - 1),
+                )
+            nc.scalar.copy(out=summed[:, :, m * SLOTS:(m + 1) * SLOTS], in_=turn[:])
 
         result = [keep.tile([P, WINDOW], F32, align_bytes=64, name="result%d" % t) for t in range(PACK)]
 
-        def window(t, s0, s1):
-            return result[t][:].indirect(tok_list[:, s0 // PER_COL:s1 // PER_COL])
+        def window(t, m, blocks):
+            return result[t][:].indirect(tok_list[:, m * SLOTS // PER_COL:(m + blocks) * SLOTS // PER_COL])
 
-        def scatter_sum(t, s0, s1):
-            nc.scalar.activation(window(t, s0, s1), gated[:, t, s0:s1], COPY)
+        def scatter_scalar(t, m, blocks):
+            nc.scalar.activation(window(t, m, blocks), summed[:, t, m * SLOTS:(m + blocks) * SLOTS], COPY)
 
-        def scatter_add(t, s0, s1, base):
-            nc.vector.tensor_tensor(window(t, s0, s1), gated[:, t, s0:s1], base, ADD)
+        def scatter_vector(t, m, blocks):
+            nc.vector.tensor_copy(window(t, m, blocks), summed[:, t, m * SLOTS:(m + blocks) * SLOTS])
 
-        for q in range(PAIRS):
-            cols = slice(q * 2 * N, (q + 1) * 2 * N)
-            gather_b_scales(q)
-            gather(nc, bg[:, cols].bitcast(U32), b_win[:].bitcast(U32), b_list, q * 2 * N, 2 * N)
-            second_layer(2 * q)
-            second_layer(2 * q + 1)
-            if q < PAIRS - 1:
-                scatter_sum(0, q * PAIR + SLOTS, (q + 1) * PAIR)
+        def scatter_add(t, m, blocks):
+            slots = slice(m * SLOTS, (m + blocks) * SLOTS)
+            nc.vector.tensor_tensor(window(t, m, blocks), summed[:, t, slots], base_high[:, t - 2, slots], ADD)
 
-        scatter_add(1, 0, PAIR, base_slot[0][:, PAIR:])
-        for q in range(PAIRS):
+        gated = [y_gated(i, 6 + i) for i in range(2)]
+
+        quantize_h(1, placed("hq1", [P, PAIR], I32, 38 * KIB))
+        gated = gated + [y_gated(2 + i, i) for i in range(2)]
+        h_grp.append(placed("h_grp2", [P, 2 * H], BF16, 57 * KIB))
+        h_turned(2, 2, nc.vector.tensor_copy)
+        b_scales(2, placed("bsg2", [P, 2 * N], U8, 56 * KIB))
+        quantize_h(2, keep.tile([P, PAIR], I32, align_bytes=64, name="hq2"))
+        bg_last = placed("bg_last", [P, 2 * N], I32, 58 * KIB)
+        for i in range(2):
+            b_words(bg_last[:, i * N:(i + 1) * N], 4 + i, 1)
+        words = words + [bg_last[:, i * N:(i + 1) * N] for i in range(2)]
+
+        for m, number in enumerate((4, 5, 3, 2)):
+            y_turned(m, gated[m], number, m < 3)
+        gated = [y_gated(4 + i, 4 + i) for i in range(2)]
+        scatter_scalar(0, 3, 1)
+        for i in range(2):
+            y_turned(4 + i, gated[i], 6 + i, True)
+
+        for m in (0, 2, 4):
             for t in (3, 2):
-                scatter_add(t, q * PAIR, (q + 1) * PAIR, base_high[:, t - 2, q * PAIR:(q + 1) * PAIR])
-        scatter_sum(0, 2 * PAIR, T)
-        scatter_sum(0, 0, SLOTS)
-        scatter_sum(0, PAIR, PAIR + SLOTS)
-        scatter_sum(1, 2 * PAIR, T)
-        scatter_sum(1, PAIR, 2 * PAIR)
+                scatter_add(t, m, 2)
+        scatter_scalar(1, 4, 2)
+        scatter_scalar(0, 4, 2)
+        scatter_scalar(1, 0, 2)
+        scatter_scalar(0, 0, 3)
+        scatter_vector(1, 2, 2)
 
         planes = keep.tile([P, PACK, T], BF16, align_bytes=64)
         out_rows = out_0.rearrange("(p t) c -> p t c", t=PACK)
-        for t in (0, 3, 1, 2):
+        for t in (3, 2, 1, 0):
             nc.sync.dma_start(out=out_rows[:, t, :], in_=result[t][:, :T])
-            if t >= 2:
+            if t >= 1:
                 nc.vector.tensor_copy(out=planes[:, t, :], in_=result[t][:, :T])
             else:
                 nc.scalar.copy(out=planes[:, t, :], in_=result[t][:, :T])

@@ -98,14 +98,14 @@ def tile_moe_dyl_none_kernel(
             asg.append(tile)
             gather(nc, asg[q][:], as_win[:], a_list, q * 2 * H, 2 * H)
 
-        for q in range(2):
+        for q in range(PAIRS):
             gather_a_scales(q, keep.tile([P, 2 * H], U8, align_bytes=64, name="asg%d" % q, tag="scales%d" % q))
 
         w_bf = keep.tile([P, N * PACK], BF16, align_bytes=64, tag="wbf_then_gate")
         for i in range(2):
             nc.scalar.copy(
-                out=w_bf[:].rearrange("p (t m j) -> p m t j", t=PACK, j=PACK)[:, i * P // 2:(i + 1) * P // 2],
-                in_=w_raw[i][:].rearrange("p j (m t) -> p m t j", t=PACK),
+                out=w_bf[:].rearrange("p (t m j) -> p m j t", t=PACK, j=PACK)[:, i * P // 2:(i + 1) * P // 2],
+                in_=w_raw[i][:].rearrange("p j (m t) -> p m j t", t=PACK),
             )
         wq = keep.tile([P, N], I32, align_bytes=64)
         wqs = keep.tile([P, N], U8, align_bytes=64)
@@ -115,7 +115,6 @@ def tile_moe_dyl_none_kernel(
         gate_col = keep.tile([P, B], F32, align_bytes=64, tag="wbf_then_gate")
         with nc.allow_non_contiguous_dma(reason="one gate value for each slot's partition"):
             nc.sync.dma_start(out=gate_col[:], in_=gate[0:1, :].rearrange("o (m u) -> u (o m)", u=SLOTS))
-        gather_a_scales(2, shared.tile([P, 2 * H], U8, align_bytes=64, name="asg2", offset=12 * 1024))
 
         def placed(name, shape, dtype, offset):
             return shared.tile(shape, dtype, align_bytes=64, name=name, offset=offset)
@@ -155,7 +154,7 @@ def tile_moe_dyl_none_kernel(
             cols = slice(q * 2 * H, (q + 1) * 2 * H)
             gather(nc, ag[:, cols].bitcast(U32), a_win[:].bitcast(U32), a_list, q * 2 * H, 2 * H)
 
-        h_grp = [placed("h_grp%d" % q, [P, 2 * H], BF16, (40 + 16 * q) * KIB) for q in range(2)]
+        h_grp = [placed("h_grp%d" % q, [P, 2 * H], BF16, (40 + 16 * q) * KIB) for q in range(PAIRS)]
         h_bf = []
 
         def h_rounded(m, number):
@@ -172,23 +171,24 @@ def tile_moe_dyl_none_kernel(
                 in_=acc[:].rearrange("s (p u e) -> s u p e", u=2, e=2),
             )
 
-        def h_turned(q, number, copy):
+        def h_turned(q, number):
             turn = bank(number, [P, 2, 2, SLOTS], "h_turn")
             for i in range(2):
                 pairs = h_bf[2 * q + i][:].bitcast(F32)
                 for u in range(2):
                     nc.tensor.transpose(turn[:, i, u, :], pairs[:, u * P:(u + 1) * P], ident[:])
-            copy(
+            nc.scalar.copy(
                 out=h_grp[q][:].bitcast(F32).rearrange("p (i s u) -> p i s u", i=2, u=2),
                 in_=turn[:].rearrange("p i u s -> p i s u"),
             )
 
         for m, number in enumerate((6, 7, 0, 1, 6)):
             h_rounded(m, number)
-        h_turned(0, 2, nc.scalar.copy)
+        h_turned(0, 2)
         h_rounded(5, 7)
-        h_turned(1, 3, nc.scalar.copy)
+        h_turned(1, 3)
         frozen_low(2, 0)
+        h_turned(2, 2)
         acc = bank(1, [P, 2, PAIR], "rest_acc")
         for u in range(2):
             frozen_high(acc[:, u, :], 2 + u, 2 * PAIR, T)
@@ -267,11 +267,9 @@ def tile_moe_dyl_none_kernel(
 
         quantize_h(1, placed("hq1", [P, PAIR], I32, 38 * KIB))
         gated = gated + [y_gated(2 + i, i) for i in range(2)]
-        h_grp.append(placed("h_grp2", [P, 2 * H], BF16, 57 * KIB))
-        h_turned(2, 2, nc.vector.tensor_copy)
         b_scales(2, placed("bsg2", [P, 2 * N], U8, 56 * KIB))
-        quantize_h(2, keep.tile([P, PAIR], I32, align_bytes=64, name="hq2"))
-        bg_last = placed("bg_last", [P, 2 * N], I32, 58 * KIB)
+        quantize_h(2, placed("hq2", [P, PAIR], I32, 57 * KIB))
+        bg_last = placed("bg_last", [P, 2 * N], I32, 72 * KIB)
         for i in range(2):
             b_words(bg_last[:, i * N:(i + 1) * N], 4 + i, 1)
         words = words + [bg_last[:, i * N:(i + 1) * N] for i in range(2)]

@@ -15,6 +15,7 @@ U8 = mybir.dt.uint8
 FP8X4 = mybir.dt.float8_e4m3fn_x4
 COPY = mybir.ActivationFunctionType.Copy
 ADD = mybir.AluOpType.add
+MULT = mybir.AluOpType.mult
 
 P = 128
 PACK = 4
@@ -122,8 +123,9 @@ def tile_moe_dyl_none_kernel(
         def bank(number, shape, name):
             return banks.tile(shape, F32, tag="bank%d" % number, name=name)
 
-        base_low = [keep.tile([P, 2, PAIR], F32, align_bytes=64, name="base_low%d" % q) for q in range(PAIRS)]
-        base_high = keep.tile([P, 2, T], F32, align_bytes=64)
+        base_low = [keep.tile([P, 2, PAIR], F32, align_bytes=64, name="base_low%d" % q) for q in range(2)]
+        base_last = keep.tile([P, 2, N], F32, align_bytes=64)
+        base_high = keep.tile([P, 2, 2 * PAIR], F32, align_bytes=64)
 
         def frozen_low(q, number):
             acc = bank(number, [P, 2, PAIR], "low_acc")
@@ -147,7 +149,16 @@ def tile_moe_dyl_none_kernel(
         for u in range(2):
             acc = bank(2 + u, [P, 2 * PAIR], "high_acc")
             frozen_high(acc[:], 2 + u, 0, 2 * PAIR)
-            nc.scalar.copy(out=base_high[:, u, :2 * PAIR], in_=acc[:])
+            nc.scalar.copy(out=base_high[:, u, :], in_=acc[:])
+
+        def frozen_last(i, number):
+            acc = bank(number, [P, N], "last_acc")
+            block = slice((4 + i) * SLOTS, (5 + i) * SLOTS)
+            nc.tensor.matmul_mx(
+                out=acc[:], lhsT=xg[:, block].bitcast(FP8X4), lhsT_scale=xsg[:, block],
+                rhs=wq[:].bitcast(FP8X4), rhs_scale=wqs[:], start=True, stop=True,
+            )
+            nc.scalar.copy(out=base_last[:, i, :], in_=acc[:])
 
         ag = shared.tile([P, B * H], I32, align_bytes=64, offset=0)
         for q in range(PAIRS):
@@ -187,12 +198,9 @@ def tile_moe_dyl_none_kernel(
         h_turned(0, 2)
         h_rounded(5, 7)
         h_turned(1, 3)
-        frozen_low(2, 0)
+        frozen_last(0, 0)
         h_turned(2, 2)
-        acc = bank(1, [P, 2, PAIR], "rest_acc")
-        for u in range(2):
-            frozen_high(acc[:, u, :], 2 + u, 2 * PAIR, T)
-        nc.scalar.copy(out=base_high[:, :, 2 * PAIR:], in_=acc[:])
+        frozen_last(1, 1)
 
         bsg = []
         hq = []
@@ -238,7 +246,10 @@ def tile_moe_dyl_none_kernel(
 
         def y_turned(m, y_sb, number, frozen_first):
             turn = bank(number, [P, PACK, SLOTS], "y_turn")
-            frozen = [(t, base_low[m // 2][:, m % 2, t * P:(t + 1) * P]) for t in range(2)]
+            if m < 4:
+                frozen = [(t, base_low[m // 2][:, m % 2, t * P:(t + 1) * P]) for t in range(2)]
+            else:
+                frozen = [(t, base_last[:, m % 2, t * P:(t + 1) * P]) for t in range(PACK)]
             adapter = [(t, y_sb[:, t, :]) for t in range(PACK)]
             terms = frozen + adapter if frozen_first else adapter + frozen
             for k, (t, term) in enumerate(terms):
@@ -281,9 +292,11 @@ def tile_moe_dyl_none_kernel(
         for i in range(2):
             y_turned(4 + i, gated[i], 6 + i, True)
 
-        for m in (0, 2, 4):
+        for m in (0, 2):
             for t in (3, 2):
                 scatter_add(t, m, 2)
+        for t in (3, 2):
+            scatter_vector(t, 4, 2)
         scatter_scalar(1, 4, 2)
         scatter_scalar(0, 4, 2)
         scatter_scalar(1, 0, 2)
@@ -294,10 +307,13 @@ def tile_moe_dyl_none_kernel(
         out_rows = out_0.rearrange("(p t) c -> p t c", t=PACK)
         for t in (3, 2, 1, 0):
             nc.sync.dma_start(out=out_rows[:, t, :], in_=result[t][:, :T])
-            if t >= 1:
+            if t >= 2:
+                nc.gpsimd.tensor_scalar(planes[:, t, :], result[t][:, :T], 1.0, -0.0, MULT, ADD)
+            elif t == 1:
                 nc.vector.tensor_copy(out=planes[:, t, :], in_=result[t][:, :T])
             else:
-                nc.scalar.copy(out=planes[:, t, :], in_=result[t][:, :T])
+                nc.vector.tensor_copy(out=planes[:, t, :T // 2], in_=result[t][:, :T // 2])
+                nc.scalar.copy(out=planes[:, t, T // 2:], in_=result[t][:, T // 2:T])
 
         C = T // 3
         out_scales = keep.tile([P, T], U8, align_bytes=64)

from contextlib import ExitStack

import concourse.mybir as mybir
from concourse.masks import make_identity

K, T, E, B, H, N = 512, 768, 8, 6, 512, 512
FLOPS = 2 * K * N * T + 2 * K * H * T + 2 * H * N * T

F32 = mybir.dt.float32
BF16 = mybir.dt.bfloat16
I32 = mybir.dt.int32
U32 = mybir.dt.uint32
U16 = mybir.dt.uint16
U8 = mybir.dt.uint8
FP8X4 = mybir.dt.float8_e4m3fn_x4
COPY = mybir.ActivationFunctionType.Copy
ADD = mybir.AluOpType.add
MULT = mybir.AluOpType.mult

P = 128
PACK = 4
SLOTS = 128
PAIR = 2 * SLOTS
PAIRS = B // 2
KIB = 1024
PER_COL = 16
WINDOW = 1024
A_ROW, B_ROW = 4, 8


def load_words(queue, tile, words):
    queue.dma_start(out=tile, in_=words[0].rearrange("p c d -> p (c d)").bitcast(I32))


def load_scale_rows(queue, plane, scales, first_row):
    rows = scales[0].bitcast(I32)
    view = plane.bitcast(I32)
    for r in range(4):
        queue.dma_start(out=view[first_row + r:P:32, :], in_=rows[r:16:4, :])


def gather(nc, out, window, offsets, first, count):
    cols = slice(first // PER_COL, (first + count) // PER_COL)
    nc.vector.tensor_copy(out, window.indirect(offsets[:, cols]))


def tile_moe_dyl_none_kernel(
    tc, x_words, x_scales, w, wa_words, wa_scales, wb_words, wb_scales, gate, offs, offs2, offs3,
    out_0, out_1, out_2,
):
    nc = tc.nc
    with ExitStack() as ctx:
        keep = ctx.enter_context(tc.tile_pool(name="keep", bufs=1))
        ring = ctx.enter_context(tc.tile_pool(name="ring", bufs=2))
        shared = ctx.enter_context(tc.tile_pool(name="shared", bufs=1))
        banks = ctx.enter_context(tc.psum_pool(name="banks", bufs=1))

        tok_list = keep.tile([P, T // PER_COL], U16)
        a_list = keep.tile([P, B * H // PER_COL], U16)
        b_list = keep.tile([P, B * N // PER_COL], U16)
        x_win = keep.tile([P, WINDOW], I32, align_bytes=64, tag="x_then_a")
        xs_win = keep.tile([P, WINDOW], U8, align_bytes=64)
        as_win = keep.tile([P, E * H], U8, align_bytes=64)
        bs_win = keep.tile([P, E * N], U8, align_bytes=64)
        w_raw = [
            shared.tile([P, PACK, N // 2], F32, align_bytes=64, name="w_raw%d" % i, offset=(15 - 4 * i) * 1024)
            for i in range(2)
        ]
        ident = keep.tile([P, P], F32, align_bytes=64)

        nc.vector.memset(xs_win[:].bitcast(I32), 0)
        nc.gpsimd.memset(as_win[:, :E * H // 2].bitcast(I32), 0)
        nc.vector.memset(as_win[:, E * H // 2:].bitcast(I32), 0)
        nc.gpsimd.memset(x_win[:, T:], 0)
        nc.vector.memset(bs_win[:].bitcast(I32), 0)
        make_identity(nc, ident[:])

        nc.sync.dma_start(tok_list[:], offs)
        load_words(nc.sync, x_win[:, :T], x_words)
        load_scale_rows(nc.sync, xs_win[:, :T], x_scales, 0)
        load_scale_rows(nc.sync, as_win[:], wa_scales, A_ROW)
        nc.sync.dma_start(a_list[:], offs2)
        w_rows = w.rearrange("(p j) n -> p j n", j=PACK)
        for i in range(2):
            nc.sync.dma_start(out=w_raw[i][:], in_=w_rows[:, :, i * N // 2:(i + 1) * N // 2])
        nc.sync.dma_start(b_list[:], offs3)
        load_scale_rows(nc.sync, bs_win[:], wb_scales, B_ROW)

        xg = keep.tile([P, T], I32, align_bytes=64)
        xsg = keep.tile([P, T], U8, align_bytes=64)
        gather(nc, xg[:].bitcast(U32), x_win[:].bitcast(U32), tok_list, 0, T)
        a_win = keep.tile([P, E * H], I32, align_bytes=64, tag="x_then_a")
        load_words(nc.sync, a_win[:], wa_words)
        gather(nc, xsg[:], xs_win[:], tok_list, 0, T)

        asg = []

        def gather_a_scales(q, tile):
            asg.append(tile)
            gather(nc, asg[q][:], as_win[:], a_list, q * 2 * H, 2 * H)

        for q in range(PAIRS):
            gather_a_scales(q, keep.tile([P, 2 * H], U8, align_bytes=64, name="asg%d" % q, tag="scales%d" % q))

        w_bf = keep.tile([P, N * PACK], BF16, align_bytes=64, tag="wbf_then_gate")
        for i in range(2):
            nc.scalar.copy(
                out=w_bf[:].rearrange("p (t m j) -> p m j t", t=PACK, j=PACK)[:, i * P // 2:(i + 1) * P // 2],
                in_=w_raw[i][:].rearrange("p j (m t) -> p m j t", t=PACK),
            )
        wq = keep.tile([P, N], I32, align_bytes=64)
        wqs = keep.tile([P, N], U8, align_bytes=64)
        nc.vector.quantize_mx(out=wq[:].bitcast(FP8X4), scales=wqs[:], in_=w_bf[:])
        b_win = shared.tile([P, E * N], I32, align_bytes=64, offset=13 * 1024)
        load_words(nc.sync, b_win[:], wb_words)
        gate_col = keep.tile([P, B], F32, align_bytes=64, tag="wbf_then_gate")
        with nc.allow_non_contiguous_dma(reason="one gate value for each slot's partition"):
            nc.sync.dma_start(out=gate_col[:], in_=gate[0:1, :].rearrange("o (m u) -> u (o m)", u=SLOTS))

        def placed(name, shape, dtype, offset):
            return shared.tile(shape, dtype, align_bytes=64, name=name, offset=offset)

        def bank(number, shape, name):
            return banks.tile(shape, F32, tag="bank%d" % number, name=name)

        base_low = [keep.tile([P, 2, PAIR], F32, align_bytes=64, name="base_low%d" % q) for q in range(2)]
        base_last = keep.tile([P, 2, N], F32, align_bytes=64)
        base_high = keep.tile([P, 2, 2 * PAIR], F32, align_bytes=64)

        def frozen_low(q, number):
            acc = bank(number, [P, 2, PAIR], "low_acc")
            for i in range(2):
                block = slice((2 * q + i) * SLOTS, (2 * q + i + 1) * SLOTS)
                nc.tensor.matmul_mx(
                    out=acc[:, i, :], lhsT=xg[:, block].bitcast(FP8X4), lhsT_scale=xsg[:, block],
                    rhs=wq[:, :2 * P].bitcast(FP8X4), rhs_scale=wqs[:, :2 * P], start=True, stop=True,
                )
            nc.scalar.copy(out=base_low[q][:], in_=acc[:])

        def frozen_high(acc, t, s0, s1):
            cols = slice(t * P, (t + 1) * P)
            nc.tensor.matmul_mx(
                out=acc, lhsT=wq[:, cols].bitcast(FP8X4), lhsT_scale=wqs[:, cols],
                rhs=xg[:, s0:s1].bitcast(FP8X4), rhs_scale=xsg[:, s0:s1], start=True, stop=True,
            )

        for q in range(2):
            frozen_low(q, q)
        for u in range(2):
            acc = bank(2 + u, [P, 2 * PAIR], "high_acc")
            frozen_high(acc[:], 2 + u, 0, 2 * PAIR)
            nc.scalar.copy(out=base_high[:, u, :], in_=acc[:])

        def frozen_last(i, number):
            acc = bank(number, [P, N], "last_acc")
            block = slice((4 + i) * SLOTS, (5 + i) * SLOTS)
            nc.tensor.matmul_mx(
                out=acc[:], lhsT=xg[:, block].bitcast(FP8X4), lhsT_scale=xsg[:, block],
                rhs=wq[:].bitcast(FP8X4), rhs_scale=wqs[:], start=True, stop=True,
            )
            nc.scalar.copy(out=base_last[:, i, :], in_=acc[:])

        ag = shared.tile([P, B * H], I32, align_bytes=64, offset=0)
        for q in range(PAIRS):
            cols = slice(q * 2 * H, (q + 1) * 2 * H)
            gather(nc, ag[:, cols].bitcast(U32), a_win[:].bitcast(U32), a_list, q * 2 * H, 2 * H)

        h_grp = [placed("h_grp%d" % q, [P, 2 * H], BF16, (40 + 16 * q) * KIB) for q in range(PAIRS)]
        h_bf = []

        def h_rounded(m, number):
            slots = slice(m * SLOTS, (m + 1) * SLOTS)
            sc = slice((m % 2) * H, (m % 2 + 1) * H)
            acc = bank(number, [P, H], "h_acc")
            nc.tensor.matmul_mx(
                out=acc[:], lhsT=xg[:, slots].bitcast(FP8X4), lhsT_scale=xsg[:, slots],
                rhs=ag[:, m * H:(m + 1) * H].bitcast(FP8X4), rhs_scale=asg[m // 2][A_ROW:, sc], start=True, stop=True,
            )
            h_bf.append(keep.tile([P, H], BF16, align_bytes=64, name="h_bf%d" % m))
            nc.scalar.copy(
                out=h_bf[m][:].rearrange("s (u p e) -> s u p e", u=2, e=2),
                in_=acc[:].rearrange("s (p u e) -> s u p e", u=2, e=2),
            )

        def h_turned(q, number):
            turn = bank(number, [P, 2, 2, SLOTS], "h_turn")
            for i in range(2):
                pairs = h_bf[2 * q + i][:].bitcast(F32)
                for u in range(2):
                    nc.tensor.transpose(turn[:, i, u, :], pairs[:, u * P:(u + 1) * P], ident[:])
            nc.scalar.copy(
                out=h_grp[q][:].bitcast(F32).rearrange("p (i s u) -> p i s u", i=2, u=2),
                in_=turn[:].rearrange("p i u s -> p i s u"),
            )

        for m, number in enumerate((6, 7, 0, 1, 6)):
            h_rounded(m, number)
        h_turned(0, 2)
        h_rounded(5, 7)
        h_turned(1, 3)
        frozen_last(0, 0)
        h_turned(2, 2)
        frozen_last(1, 1)

        bsg = []
        hq = []

        def b_scales(q, tile):
            gather(nc, tile[:], bs_win[:], b_list, q * 2 * N, 2 * N)
            bsg.append(tile)

        def b_words(out, m, blocks):
            gather(nc, out.bitcast(U32), b_win[:].bitcast(U32), b_list, m * N, blocks * N)

        def quantize_h(q, codes):
            scales = keep.tile([P, PAIR], U8, align_bytes=64, name="hqs%d" % q)
            nc.vector.quantize_mx(out=codes[:].bitcast(FP8X4), scales=scales[:], in_=h_grp[q][:])
            hq.append((codes, scales))

        for q in range(2):
            b_scales(q, keep.tile([P, 2 * N], U8, align_bytes=64, name="bsg%d" % q, tag="scales%d" % q))
        quantize_h(0, keep.tile([P, PAIR], I32, align_bytes=64, name="hq0"))
        bg0 = placed("bg0", [P, N], I32, 38 * KIB + 512)
        b_words(bg0[:], 0, 1)
        bg_mid = placed("bg_mid", [P, 3 * N], I32, 41 * KIB)
        b_words(bg_mid[:, :N], 1, 1)
        b_words(bg_mid[:, N:], 2, 2)
        words = [bg0[:]] + [bg_mid[:, i * N:(i + 1) * N] for i in range(3)]

        summed = keep.tile([P, PACK, T], F32, align_bytes=64)

        def y_gated(m, number):
            sc = slice((m % 2) * N, (m % 2 + 1) * N)
            hc = slice((m % 2) * SLOTS, (m % 2 + 1) * SLOTS)
            acc = bank(number, [P, N], "y_acc")
            nc.tensor.matmul_mx(
                out=acc[:], lhsT=hq[m // 2][0][:, hc].bitcast(FP8X4), lhsT_scale=hq[m // 2][1][:, hc],
                rhs=words[m].bitcast(FP8X4), rhs_scale=bsg[m // 2][B_ROW:, sc], start=True, stop=True,
            )
            y_sb = ring.tile([P, PACK, P], F32, align_bytes=64, bufs=4)
            nc.scalar.activation(
                out=y_sb[:], in_=acc[:].rearrange("s (p t) -> s t p", t=PACK), func=COPY,
                scale=gate_col[:, m:m + 1],
            )
            return y_sb

        def y_turned(m, y_sb, number, frozen_first):
            turn = bank(number, [P, PACK, SLOTS], "y_turn")
            if m < 4:
                frozen = [(t, base_low[m // 2][:, m % 2, t * P:(t + 1) * P]) for t in range(2)]
            else:
                frozen = [(t, base_last[:, m % 2, t * P:(t + 1) * P]) for t in range(PACK)]
            adapter = [(t, y_sb[:, t, :]) for t in range(PACK)]
            terms = frozen + adapter if frozen_first else adapter + frozen
            for k, (t, term) in enumerate(terms):
                nc.tensor.matmul(
                    turn[:, t, :], lhsT=term, rhs=ident[:], is_transpose=True,
                    start=(k == 0), stop=(k == len(terms) - 1),
                )
            nc.scalar.copy(out=summed[:, :, m * SLOTS:(m + 1) * SLOTS], in_=turn[:])

        result = [keep.tile([P, WINDOW], F32, align_bytes=64, name="result%d" % t) for t in range(PACK)]

        def window(t, m, blocks):
            return result[t][:].indirect(tok_list[:, m * SLOTS // PER_COL:(m + blocks) * SLOTS // PER_COL])

        def scatter_scalar(t, m, blocks):
            nc.scalar.activation(window(t, m, blocks), summed[:, t, m * SLOTS:(m + blocks) * SLOTS], COPY)

        def scatter_vector(t, m, blocks):
            nc.vector.tensor_copy(window(t, m, blocks), summed[:, t, m * SLOTS:(m + blocks) * SLOTS])

        def scatter_add(t, m, blocks):
            slots = slice(m * SLOTS, (m + blocks) * SLOTS)
            nc.vector.tensor_tensor(window(t, m, blocks), summed[:, t, slots], base_high[:, t - 2, slots], ADD)

        gated = [y_gated(i, 6 + i) for i in range(2)]

        quantize_h(1, placed("hq1", [P, PAIR], I32, 38 * KIB))
        gated = gated + [y_gated(2 + i, i) for i in range(2)]
        b_scales(2, placed("bsg2", [P, 2 * N], U8, 56 * KIB))
        quantize_h(2, placed("hq2", [P, PAIR], I32, 57 * KIB))
        bg_last = placed("bg_last", [P, 2 * N], I32, 72 * KIB)
        for i in range(2):
            b_words(bg_last[:, i * N:(i + 1) * N], 4 + i, 1)
        words = words + [bg_last[:, i * N:(i + 1) * N] for i in range(2)]

        for m, number in enumerate((4, 5, 3, 2)):
            y_turned(m, gated[m], number, m < 3)
        gated = [y_gated(4 + i, 4 + i) for i in range(2)]
        scatter_scalar(0, 3, 1)
        for i in range(2):
            y_turned(4 + i, gated[i], 6 + i, True)

        for m in (0, 2):
            for t in (3, 2):
                scatter_add(t, m, 2)
        for t in (3, 2):
            scatter_vector(t, 4, 2)
        scatter_scalar(1, 4, 2)
        scatter_scalar(0, 4, 2)
        scatter_scalar(1, 0, 2)
        scatter_scalar(0, 0, 3)
        scatter_vector(1, 2, 2)

        planes = keep.tile([P, PACK, T], BF16, align_bytes=64)
        out_rows = out_0.rearrange("(p t) c -> p t c", t=PACK)
        for t in (3, 2, 1, 0):
            nc.sync.dma_start(out=out_rows[:, t, :], in_=result[t][:, :T])
            if t >= 2:
                nc.gpsimd.tensor_scalar(planes[:, t, :], result[t][:, :T], 1.0, -0.0, MULT, ADD)
            elif t == 1:
                nc.vector.tensor_copy(out=planes[:, t, :], in_=result[t][:, :T])
            else:
                nc.vector.tensor_copy(out=planes[:, t, :T // 2], in_=result[t][:, :T // 2])
                nc.scalar.copy(out=planes[:, t, T // 2:], in_=result[t][:, T // 2:T])

        C = T // 3
        out_scales = keep.tile([P, T], U8, align_bytes=64)
        out_words = out_1[0].rearrange("p c d -> p (c d)").bitcast(I32)
        woven = [keep.tile([P, C, PACK], BF16, align_bytes=64, name="woven%d" % c) for c in range(3)]
        for c in range(3):
            src = planes[:, :, c * C:(c + 1) * C].rearrange("p t (c i) -> p c t i", i=4)
            dst = woven[c][:].rearrange("p (c i) t -> p c t i", i=4)
            if c == 2:
                nc.scalar.copy(out=dst, in_=src)
            else:
                nc.vector.tensor_copy(out=dst, in_=src)
        for c in range(3):
            codes = keep.tile([P, C], I32, align_bytes=64, name="codes%d" % c)
            nc.vector.quantize_mx(
                out=codes[:].bitcast(FP8X4), scales=out_scales[:, c * C:(c + 1) * C],
                in_=woven[c][:].rearrange("p c t -> p (c t)"),
            )
            nc.sync.dma_start(out=out_words[:, c * C:(c + 1) * C], in_=codes[:])
        scale_rows = out_2[0].bitcast(I32)
        for quad in range(4):
            queue = nc.sync if quad % 2 == 0 else nc.scalar
            queue.dma_start(
                out=scale_rows[4 * quad:4 * quad + 4, :],
                in_=out_scales[:].bitcast(I32)[32 * quad:32 * quad + 4, :],
            )
